import numpy as np, ml_dtypes
CORES = [25,29,65,69,153,157,193,197]
N = 8
BF = ml_dtypes.bfloat16
M, L, CAP, VI, ST = 2304, 208, 160, 3, 5
W = M + (VI - 1) * L
def weights(rng):
    w = rng.integers(0, 64, (N, 8, 16)); o = np.argsort(rng.random((N, 8, 16)), axis=-1)
    a = o[..., :1] == np.arange(16); b = o[..., 1:2] == np.arange(16)
    return np.where(a, 1, np.where(b, 16, w)), a[:, :, None], b[:, :, None]
def aim(v, w, a, b, t):
    v = np.where(a | b, 0, v); need = (t - np.sum(v * w[:, :, None], axis=-1)) & 63
    return v + a * (need & 15)[..., None] + b * (need >> 4)[..., None]
def shake(rng, v, k, top):
    return np.clip(v + np.floor((2 * k + 1) * rng.random(v.shape)).astype(np.int64) - k, 0, top)
def homes(rng, e):
    t = (64 * rng.random((N, 8, M)) ** e).astype(np.int64)
    t = (t * (2 * rng.integers(0, 32, (N, 8, 1)) + 1) + rng.integers(0, 64, (N, 8, 1))) & 63
    t[:, :, 1:65] = np.arange(64); return t
def points(rng, w, a, b, top):
    tree = homes(rng, rng.choice(np.array([1.0, 1.5, 2.0, 3.0]), (N, 8, 1)))
    mid = rng.integers(0, top + 1, (N, 8, 64, 16)); k = rng.integers(0, 9, (N, 8, M, 1)); k[:, :, 1:65] = 0
    v = shake(rng, np.take_along_axis(mid, tree[..., None], 2), k, top)
    far = rng.random((N, 8, M, 1)) < 0.3; far[:, :, 1:65] = False
    return tree, aim(np.where(far, rng.integers(0, top + 1, v.shape), v), w, a, b, tree)
def grow(v, tree):
    x = v.astype(np.int32); c = np.zeros(N * 8 * M * 16, np.int64)
    R, g, n = np.nonzero(np.broadcast_to(np.arange(M) > 64, (N, 8, M))); at = tree[R, g, n] + 1
    for _ in range(24):
        if len(n) == 0: break
        band = np.add.reduce(np.abs(x[R, g, n] - x[R, g, at]), axis=-1) >> 4
        key = ((R * 8 + g) * M + at) * 16 + band
        u, i = np.unique(key, return_index=True); c[u] = n[i]
        more = np.ones(len(n), bool); more[i] = False
        R, g, n, at = R[more], g[more], n[more], c[key[more]]
    return c.reshape(N, 8, M, 16)
def queries(rng, v, tree, w, a, b):
    o = rng.integers(1, M, (N, 8, VI * L)); k = rng.integers(0, 7, (N, 8, VI * L, 1))
    s = shake(rng, np.take_along_axis(v, o[..., None], 2), k, 15)
    s = np.where(rng.random((N, 8, VI * L, 1)) < 0.25, rng.integers(0, 16, s.shape), s)
    return aim(s, w, a, b, np.take_along_axis(tree, o, 2))
def radii(rng):
    z = (N, 8, VI * L)
    return np.where(rng.random(z) < 0.7, rng.integers(100, 256, z), rng.integers(0, 100, z))
def full(v):
    return np.ascontiguousarray(v.transpose(0, 1, 3, 2)).reshape(N, 128, -1)
def pack(v, c, s, w, r0, th):
    return {"pt": full(v).astype(np.float32).astype(BF), "ch": full(c).astype(np.int32), "q": full(s).astype(np.float32).astype(BF),
            "w": np.ascontiguousarray(w.reshape(N, 128, 1)).astype(np.int32), "r0": r0.astype(np.int32), "th": np.repeat(th, 16, axis=1)[..., None].astype(np.int32)}
def setup_inputs(rng):
    w, a, b = weights(rng); tree, v = points(rng, w, a, b, 15)
    return pack(v, grow(v, tree), queries(rng, v, tree, w, a, b), w, radii(rng), rng.integers(20, 60, (N, 8)))
def setup_inputs_room(rng):
    w, a, b = weights(rng); tree, v = points(rng, w, a, b, 10); z = (N, 8, VI * L)
    n = rng.choice(np.array([0, 1, CAP - 1, CAP, CAP + 1, L]), (N, 8)); n[0] = (CAP, CAP + 1, L, CAP - 1, 1, 0, CAP, CAP + 1); n[:, 2] = L
    n = np.concatenate([n[:, :, None], np.full((N, 8, VI - 1), L // 2)], axis=2)
    hot = (np.argsort(rng.random((N, 8, VI, L)), axis=-1) < n[..., None]).reshape(z)
    s = np.where(hot[..., None], rng.integers(12, 16, z + (16,)), queries(rng, v, tree, w, a, b))
    r0 = np.where(hot, rng.choice(np.array([20, 21, 255, 255, 255]), z), rng.integers(0, 20, z))
    return pack(v, grow(v, tree), s, w, r0, np.full((N, 8), 20))
def setup_inputs_knots(rng):
    w, a, b = weights(rng); v = rng.integers(0, 16, (N, 8, M, 16)); v[:, 1::2] = v[:, 1::2][:, :, rng.integers(0, 37, M)]
    dens = rng.choice(np.array([1.0, 0.6, 0.2]), (N, 8, 1, 1)); dens[:, 0] = 1.0; dens[:, 1] = 0.2; dens[:, 2] = 0.3
    c = np.where(rng.random((N, 8, M, 16)) < dens, rng.integers(1, M, (N, 8, M, 16)), 0)
    c[:, 3] = rng.choice(np.array([0, 1, 64, 65, M - 1]), (N, M, 16))
    c[:, 5] = np.where(rng.random((N, M, 16)) < 0.5, np.arange(M)[:, None], c[:, 5])
    x = rng.integers(1, M, (N, M, 2)); e = np.arange(16) - rng.integers(1, 6, (N, M, 1)); j = rng.choice(np.array([-1, 3, 4]), (N, M, 1))
    some = rng.random((N, M, 1)) < 0.4; some[:, 1:65] = True
    c[:, 6] = some * np.where((e >= 0) & (e < 3), x[:, :, :1], np.where(e == j, x[:, :, 1:], 0)); c[:, :, 0] = 0
    return pack(v, c, queries(rng, v, rng.integers(0, 64, (N, 8, M)), w, a, b), w, radii(rng), rng.integers(20, 80, (N, 8)))
def setup_inputs_ties(rng):
    w = rng.integers(0, 64, (N, 8, 16)); v = 4 * rng.integers(0, 4, (N, 8, M, 16)); tree = homes(rng, 1.0); z = (N, 8, VI * L)
    s = np.take_along_axis(v, rng.integers(1, M, z)[..., None], 2); s = np.where(rng.random(s.shape) < 0.3, 4 * rng.integers(0, 4, s.shape), s)
    s = np.where(rng.random(s.shape) < 0.01, 15, s); s[:, ::2, 1::2] = s[:, ::2, ::2]
    r0 = np.where(rng.random(z) < 0.4, 16 * rng.integers(3, 9, z) + rng.choice(np.array([-1, 1]), z), 4 * rng.integers(10, 40, z))
    return pack(v, grow(v, tree), s, w, r0, 4 * rng.integers(8, 15, (N, 8)))
def setup_inputs_ends(rng):
    w, a, b = weights(rng); tree, v = points(rng, w, a, b, 15); n = np.arange(L)
    v[:, 4, 65:65 + L] = rng.integers(0, 16, (N, L, 16)); tree[:, 4, 65:65 + L] = n & 63; v = aim(v, w, a, b, tree)
    s = queries(rng, v, tree, w, a, b); s[:, 4, :L] = v[:, 4, 65:65 + L]
    w[:, 1] = 0; w[:, 2] = 63; v[:, :, 1] = 0; v[:, :, 64] = 15; v[:, :, M - 1] = 15; v[:, 3, 1:65] = 0
    c = grow(v, tree); c[:, :, 1, 15] = M - 1; c[:, 3] = 0; c[:, 4, 65:] = 0; c[:, 4, 1 + (n & 63), 4 * (n >> 6) + 2] = 65 + n
    R = np.arange(N); z = 1 + ((15 * np.sum(w[:, 7], axis=-1)) & 63)
    v[R, 7, z] = 0; v[:, 7, 65] = 0; v[:, 7, 66] = 15
    c[R, 7, z] = 0; c[R, 7, z, 9] = 65; c[:, 7, 65] = 0; c[:, 7, 65, 4] = 66
    s[:, 1, ::3] = 15; s[:, 3, ::2] = 15; s[:, 3, 1::4] = rng.integers(14, 16, s[:, 3, 1::4].shape); s[:, 7, ::4] = 15
    s[:, :, 0] = 15; s[:, :, L - 1] = 0
    r0 = rng.choice(np.array([0, 1, 15, 16, 17, 120, 254, 255]), (N, 8, VI * L)); high = np.array([240, 241, 255])
    r0[:, 3, ::2] = rng.choice(high, r0[:, 3, ::2].shape); r0[:, 3, 1::4] = rng.choice(np.array([191, 192, 239, 240, 241, 255]), r0[:, 3, 1::4].shape)
    r0[:, 4, :L] = 255; r0[:, 7, ::4] = rng.choice(high, r0[:, 7, ::4].shape); r0[:, :, 0] = 255; r0[:, :, L - 1] = 255
    th = rng.choice(np.array([0, 1, 16, 30, 240]), (N, 8)); th[:, 0] = 0; th[:, 3] = np.array([0, 240, 241, 255])[R & 3]; th[:, 4] = 0; th[:, 5] = 255; th[:, 6] = 240
    return pack(v, c, s, w, r0, th)
def setup_inputs_spread(rng):
    w = rng.integers(0, 64, (N, 8, 16)); e = rng.choice(np.array([0.25, 0.5, 1.0, 2.0, 4.0]), (N, 8, 1, 16))
    v = (16 * rng.random((N, 8, M, 16)) ** e).astype(np.int64); s = (16 * rng.random((N, 8, VI * L, 16)) ** e).astype(np.int64)
    c = grow(v, homes(rng, 4.0)); c = np.where(rng.random(c.shape) < 0.1, rng.integers(0, M, c.shape), c); c[:, :, 0] = 0
    th = np.exp2(7 * rng.random((N, 8))).astype(np.int64); th[:, 0] = 8
    return pack(np.clip(v, 0, 15), c, np.clip(s, 0, 15), w, rng.integers(0, 256, (N, 8, VI * L)), th)
def check_inputs(d):
    bad = []
    for k in ("pt", "q"):
        x = np.asarray(d[k]).astype(np.float32)
        if not (np.all(x >= 0) and np.all(x <= 15) and np.all(x == np.floor(x))): bad.append("whole numbers from 0 to 15 in " + k)
    for k, hi in (("ch", M - 1), ("w", 63), ("r0", 255), ("th", 255)):
        if np.min(d[k]) < 0 or np.max(d[k]) > hi: bad.append("range of " + k)
    if np.any(np.asarray(d["ch"])[:, :, 0] != 0): bad.append("column 0 of ch")
    x = np.asarray(d["th"]).reshape(-1, 16)
    if np.any(x != x[:, :1]): bad.append("one threshold a group")
    return bad
def dist(u, v):
    return np.add.reduce(np.abs(u - v), axis=-1)
def inside(D, rho):
    i = np.arange(16); return (16 * i <= (D + rho)[..., None]) & (16 * i + 15 >= (D - rho)[..., None])
def at(k, i):
    return np.take_along_axis(k, i[..., None], -1)[..., 0]
def reference(pt, ch, q, w, r0, th):
    X = np.zeros((N, 8, W, 16), np.int32); X[:, :, :M] = pt.astype(np.float32).astype(np.int32).reshape(N, 8, 16, M).transpose(0, 1, 3, 2)
    C = np.zeros((N, 8, W, 16), np.int32); C[:, :, :M] = ch.reshape(N, 8, 16, M).transpose(0, 1, 3, 2)
    Q = np.ascontiguousarray(q.astype(np.float32).astype(np.int32).reshape(N, 8, 16, VI * L).transpose(0, 1, 3, 2))
    wt = w.astype(np.int32).reshape(N, 8, 1, 16); lim = th.reshape(N, 8, 16)[:, :, :1]
    a, b, ln = np.ogrid[0:N, 0:8, 0:L]; far_off = 1000
    yr, yb, yp, held = [], [], [], None
    for t in range(VI):
        v = np.array(Q[:, :, t * L:(t + 1) * L]); rho = np.array(r0[:, :, t * L:(t + 1) * L]).astype(np.int32); best = np.zeros((N, 8, L), np.int32)
        if held is not None:
            hv, hr, hb, sent, place = held; h = np.nonzero(sent); to = ((h[0] + 1) % N, h[1], place[h])
            v[to] = hv[h]; rho[to] = hr[h]; best[to] = hb[h]
        kid = np.zeros((N, 8, ST + 1, L, 16), np.int32); far = np.zeros((N, 8, ST + 1, L, 16), np.int32); own = np.zeros((N, 8, ST + 1, L), np.int32)
        lev = np.zeros((N, 8, L), np.int64); push = np.ones((N, 8, L), bool)
        m = 1 + (np.add.reduce(wt * v, axis=-1) & 63); D = dist(X[a, b, m], v)
        for s in range(ST + 1):
            if s > 0:
                k = kid[a, b, lev, ln]; f = far[a, b, lev, ln]; ok = (k > 0) & inside(own[a, b, lev, ln], rho)
                i = np.argmin(np.where(ok, f, far_off), axis=-1); push = np.any(ok, axis=-1)
                m = np.where(push, at(k, i), 0); D = np.where(push, at(f, i), far_off)
                h = np.nonzero(push); kid[h[0], h[1], lev[h], h[2], i[h]] = 0
                lev = np.where(push, lev + 1, np.maximum(lev - 1, 0))
            P = np.where(inside(D, rho) & push[..., None], C[a, b, m], 0)
            F = dist(X[a[..., None], b[..., None], P], v[:, :, :, None])
            h = np.nonzero(push); e = (h[0], h[1], lev[h], h[2])
            kid[e] = P[h]; far[e] = F[h]; own[e] = D[h]
            key = np.concatenate([D[..., None], np.where(P > 0, F, far_off)], axis=-1); node = np.concatenate([m[..., None], P], axis=-1)
            i = np.argmin(key, axis=-1); least = at(key, i); better = least < rho
            best = np.where(better, 4096 * a + at(node, i), best); rho = np.where(better, least, rho)
        yr.append(rho); yb.append(best)
        if t == VI - 1: break
        goes = rho >= lim; here = (best > 0) & (best >> 12 == a); node = np.where(here, best & 4095, 0); row = rho >> 4
        can = goes & here & (C[a, b, node, row] == 0)
        earlier = np.arange(L)[None, :] < np.arange(L)[:, None]
        win = can & ~np.any((node[:, :, :, None] == node[:, :, None, :]) & can[:, :, None, :] & earlier, axis=-1)
        X[:, :, M + t * L:M + (t + 1) * L] = v; h = np.nonzero(win); C[h[0], h[1], node[h], row[h]] = M + t * L + h[2]
        yp.append(np.where(win, node, 0))
        place = np.add.accumulate(goes.astype(np.int64), axis=2) - 1
        held = (v, rho, best, goes & (place < CAP), place)
    return {"yr": np.concatenate(yr, axis=2).astype(np.float32), "yb": np.concatenate(yb, axis=2).astype(np.float32), "yp": np.concatenate(yp, axis=2).astype(np.float32)}

@@ -1,0 +1,709 @@
+from concourse.bass import DstId, RemoteDMATransfer
+from concourse.mybir import AluOpType as OP, AxisListType, ActivationFunctionType as AF
+
+M, L, CAP, VI, ST = 2304, 208, 160, 3, 5
+W = M + (VI - 1) * L
+CW = W + L
+NL, K0 = (112, 96), (0, 112)
+TOP = 16777216
+CYC = 0.00083
+VS = {0: ((0, 28), (28, 56)), 1: ((0, 24), (24, 48))}
+SS = {0: ((56, 84), (84, 112)), 1: ((48, 72), (72, 96))}
+TRIES = [(0.3 * b, 0.3 * (s > 1), 1e-9, s) for b in range(12) for s in range(1, 12)]
+
+SCRATCH = {"PT": ("sbuf", [128, W], "bfloat16"), "QA": ("sbuf", [128, VI * L], "bfloat16"), "CH": ("sbuf", [128, CW], "float32"),
+           "CHI": ("sbuf", [128, CW], "int32"), "WI": ("sbuf", [128, 1], "int32"), "THI": ("sbuf", [128, 1], "int32"),
+           "Q16": ("sbuf", [128, 16 * L], "bfloat16"), "R0I": ("sbuf", [8, VI * L], "int32"),
+           "R0F": ("sbuf", [8, VI * L], "float32"), "YO": ("sbuf", [16, VI * L], "float32"), "YPO": ("sbuf", [8, 2 * L], "float32")}
+for _h in ("0", "1"):
+    SCRATCH["SEND" + _h] = ("sbuf", [128, 736], "bfloat16")
+    SCRATCH["LAND" + _h] = ("sbuf", [128, 2 * CAP], "bfloat16")
+    for _n in ("KEY", "ZB", "FB", "SP"):
+        SCRATCH[_n + _h] = ("psum", [128, 512], "float32")
+PSUMS = {n for n in SCRATCH if SCRATCH[n][0] == "psum"}
+SIZES = {n: (SCRATCH[n][1], SCRATCH[n][2]) for n in SCRATCH}
+POOL = {}
+
+
+def _pool(dtype, halves, **bufs):
+    big, at = "ALL" + dtype[0], 0
+    for two, group in ((False, bufs), (True, halves)):
+        for k in group:
+            for name in ([k + "_0", k + "_1"] if two else [k]):
+                POOL[name] = (big, at)
+                SIZES[name] = ([128, group[k]], dtype)
+                at += (group[k] + 15) // 16 * 16
+    SCRATCH[big] = ("sbuf", [128, at], dtype)
+
+
+_pool("bfloat16", dict(DT=1792, A0=112, ST=16, ST0=112, ST1=112, ST2=112, ST3=112, U=256, UF=256, UG=256, EA=128, EB=128, EC=128,
+                       ED=128), THB=128, ONB=128, IB=128, I25=128, IN=128, R8=8, W8=8, ZC=896, TRI=128, TRP=320, B5=128, MW=24,
+      SELA=8 * L, FAR=16, ML=256, MG=L, MGN=L, EE=L, FM=CAP, FQ=CAP, QF1=2 * L, XG0=512, XG1=512, QC1=L, QC2=L)
+_pool("float32", dict(PF=112, SC1=128, SC2=128, FS=128, FS2=128, NR=8, X=128, Y=128, LB=128, FC=8, FV=8, FX=8, R0S=24, KM0=128,
+                      KM1=128, KM2=128, KM3=128, PA=8, PB=8, PC=8), WF=1, THF=1, ONF=128, IF=128, ICOL=1, C4K=1, LMASK=128,
+      CMASK=8, SEGR=128, KC=16, KJ=16, KN=L, TH=8, LD0=128, LF=128, LS=128, NB=16, PM_=16, S0=16, DA=16, DB=16, DST=16, NOD=16,
+      E1=16, BST=16, OUTL=32, GG=L, OB=L, BN=L, CAN=16, DMIN=16, YPL=16, NF=16)
+_pool("int32", dict(SEL=8, ND=8, RBC=8), PI=2, RI=128, BCI=16, H=128, LW=128, SI=32, BEST=16, MI=256, MCI=256, NCI=16)
+_pool("uint16", dict(P16=112, LT=8), BCL=8, BCS=8, DL=14, NLT=14, DL2=14)
+SEMAPHORES = ["cv", "cs", "ct", "cg", "arr0", "arr1", "loc0", "loc1"] + ["d%d" % i for i in range(16)]
+PLAN = {}
+
+
+def hop_of(src, dst, cores, topo):
+    if topo.may_write(src, dst):
+        return dst
+    fit = [c for c in topo.cores_of(src) if c not in cores and topo.may_write(c, dst)]
+    return ([c for c in fit if topo.die(c) == topo.die(src)] or fit)[0]
+
+
+def some(engines, n):
+    return [sum(1 << e for e in engines[i * n:(i + 1) * n]) for i in range(len(engines) // n)]
+
+
+def rank_program(g, core, T, topo):
+    rank = T.rank_of(core)
+    cores = list(T.cores)
+    n = len(cores)
+    if rank is None:
+        for r in range(n):
+            src, dst = cores[r], cores[(r + 1) % n]
+            if hop_of(src, dst, cores, topo) == core:
+                rid, pid = topo.addr(dst, core)
+                for t in ("0", "1"):
+                    g.wait_ge(T.sem["arr" + t], 8)
+                    g.remote_dma(T["LAND" + t][:], T["LAND" + t][:], T.sem["arr" + t], T.sem["loc" + t], pid, rid,
+                                 some(topo.engines(core, dst), 8)[0])
+                for t in ("0", "1"):
+                    g.wait_ge(T.sem["loc" + t], 8)
+        return
+
+    ops, half, ndma, turn = [], [0], [0], [0]
+    QUE = {"v": g.vector, "s": g.scalar, "t": g.tensor, "g": g, "y": g.sync}
+    SEM = {"v": T.sem.cv, "s": T.sem.cs, "t": T.sem.ct, "g": T.sem.cg}
+
+    def A(name, c0=0, c1=None, st=1, p=(0, None)):
+        shp, (b, o) = SIZES[name][0], POOL.get(name, (name, 0))
+        c1 = shp[1] if c1 is None else c1
+        p1 = shp[0] if p[1] is None else p[1]
+        x = T[b][p[0]:p1, o + c0:o + c1:st] if st > 1 else T[b][p[0]:p1, o + c0:o + c1]
+        return (x, name, p[0], p1, c0, c1, st)
+
+    def ind(win, off):
+        return ("I", win, off)
+
+    def is_ind(x):
+        return isinstance(x[0], str)
+
+    def ap(x):
+        return x[1][0].indirect(x[2][0]) if is_ind(x) else x[0]
+
+    def size(x):
+        return 16 * (x[2][5] - x[2][4]) if is_ind(x) else (x[5] - x[4] + x[6] - 1) // x[6]
+
+    def cost(q, what, out, ins):
+        m = size(out)
+        if q == "v":
+            if is_ind(out):
+                return 0.05 + m * 3.5 * CYC
+            if any(is_ind(x) for x in ins):
+                return 0.05 + m * 1.5 * CYC
+            if what == "tt":
+                m *= 1 if any(x[1] in PSUMS for x in ins) else 2
+            elif what == "red":
+                m = size(ins[0])
+            elif what != "scan" and all(SIZES[x[1]][1] in ("bfloat16", "uint16") for x in [out] + list(ins)):
+                m *= 0.5
+            return max(64, m) * CYC
+        if q == "s":
+            return 0.065 + m * (1.5 if is_ind(ins[0]) else 1) * CYC
+        if q == "t":
+            return max(min(64, size(ins[0])), m) * 0.0005 * (4 if SIZES[ins[0][1]][1] == "float32" else 1)
+        return 0.15 + 2 * m * CYC
+
+    def op(q, fn, rd, wr, kind="c", sem=None, val=1, c=0.1):
+        R, Wr = [], []
+        for x in rd:
+            R += [x[1], x[2]] if is_ind(x) else [x]
+        for x in wr:
+            Wr.append(x[1] if is_ind(x) else x)
+            if is_ind(x):
+                R.append(x[2])
+        ops.append((q, fn, R, Wr, kind, sem, val, c, half[0]))
+
+    def call(q, what, fn, out, *ins):
+        op(q, fn, ins, [out], c=cost(q, what, out, ins))
+
+    def dma(q, out, in_, rd, wr):
+        s = T.sem["d%d" % ndma[0]]
+        ndma[0] += 1
+        op(q, lambda: QUE[q].dma_start(out, in_), rd, wr, "d", s, 16)
+
+    def load(q, name, src, a=0, b=None):
+        dma(q, A(name, a, b)[0], src, [], [A(name, a, b)])
+
+    def tt(out, a, b, o):
+        call("v", "tt", lambda: g.vector.tensor_tensor(ap(out), ap(a), ap(b), o), out, a, b)
+
+    def ts(out, a, s1, o0, s2=None, o1=None):
+        rd = [a] + [x for x in (s1, s2) if isinstance(x, tuple)]
+        v1, v2 = (ap(x) if isinstance(x, tuple) else x for x in (s1, s2))
+        more = () if o1 is None else (o1,)
+        op("v", lambda: g.vector.tensor_scalar(ap(out), ap(a), v1, v2, o0, *more), rd, [out], c=cost("v", "ts", out, [a]))
+
+    def cp(out, a):
+        call("v", "cp", lambda: g.vector.tensor_copy(ap(out), ap(a)), out, a)
+
+    def fill(out, c):
+        call("v", "fill", lambda: g.vector.memset(ap(out), c), out)
+
+    def scan(out, d0, d1, o0, o1):
+        call("v", "scan", lambda: g.vector.tensor_tensor_scan(ap(out), ap(d0), ap(d1), 0.0, o0, o1), out, d0, d1)
+
+    def least(out, a):
+        call("v", "red", lambda: g.vector.tensor_reduce(ap(out), ap(a), AxisListType.X, OP.min, apply_absolute_value=True), out, a)
+
+    def act(out, a, f, scale=1.0):
+        call("s", "", lambda: g.scalar.activation(ap(out), ap(a), f, scale=scale), out, a)
+
+    def mm(out, l, r, start=True, stop=True):
+        call("t", "", lambda: g.tensor.matmul(ap(out), ap(l), ap(r), start, stop), out, l, r)
+
+    def iota(out, pat, base, cm, small=False):
+        kw = {"allow_small_or_imprecise_dtypes": True} if small else {}
+        call("g", "", lambda: g.iota(ap(out), pat, base, cm, **kw), out)
+
+    def asel(out, a, pat, cmp, fillv, base, cm):
+        call("g", "", lambda: g.affine_select(ap(out), ap(a), pat, cmp, fillv, base, cm), out, a)
+
+    load("y", "WI", T.w[:])
+    load("y", "QA", T.q[:, 0:L], 0, L)
+    load("s", "R0I", T.r0[:])
+    load("s", "CHI", T.ch[:, 0:1152], 0, 1152)
+    load("y", "PT", T.pt[:], 0, M)
+    load("s", "CHI", T.ch[:, 1152:M], 1152, M)
+    load("y", "THI", T.th[:])
+    load("y", "QA", T.q[:, L:VI * L], L, VI * L)
+
+    fill(A("R8"), 65536.0)
+    fill(A("ONF"), 1.0)
+    fill(A("ONB"), 1.0)
+    fill(A("SEGR"), 0.0)
+    fill(A("ZC"), 0.0)
+    iota(A("PI", 0, 1), [[0, 1]], 0, 1)
+    iota(A("RI"), [[0, 8], [1, 16]], 0, 0)
+    asel(A("R8"), A("R8"), [[-16, 8]], OP.is_ge, 0.0, 0, 1)
+    asel(A("R8"), A("R8"), [[16, 8]], OP.is_ge, 0.0, 15, -1)
+    asel(A("CMASK"), A("ONF", 0, 8), [[-16, 8]], OP.is_ge, 0.0, 0, 1)
+    asel(A("CMASK"), A("CMASK"), [[16, 8]], OP.is_ge, 0.0, 15, -1)
+    iota(A("BCI", 0, 8), [[1, 8]], 0, 0)
+    iota(A("BCI", 8, 16), [[16, 8]], 15, 0)
+    asel(A("IF"), A("ONF"), [[-1, 128]], OP.is_equal, 0.0, 0, 1)
+    asel(A("IB"), A("ONB"), [[-1, 128]], OP.is_equal, 0.0, 0, 1)
+    Z = lambda b: A("ZC", b * 128, b * 128 + 128)
+    for b in (1, 2, 5, 6):
+        asel(Z(b), Z(b), [[-1, 8], [0, 16]], OP.not_equal, -1.0, -8, 1)
+    for b, c in ((0, 1.0), (1, -1.0), (2, 1.0), (3, -1.0), (4, 1.0)):
+        asel(Z(b), Z(b), [[-1, 8], [0, 16]], OP.not_equal, c, 0, 1)
+    for b, sgn, c in ((0, -16, -7.5), (1, 16, 0.0), (2, -16, -15.0)):
+        z = A("ZC", b * 128, b * 128 + 128, 1, (32, 34))
+        iota(z, [[0, 8], [sgn, 16]], 0, 0, True)
+        asel(z, z, [[0, 128]], OP.not_equal, c, -1, 1)
+    cp(A("ZC", 640, 896, 1, (32, 34)), A("ZC", 128, 384, 1, (32, 34)))
+    asel(A("SEGR"), A("SEGR"), [[0, 8], [1, 16]], OP.not_equal, 2147483648.0, 0, 0)
+    ts(A("PI", 1, 2), A("PI", 0, 1), 15, OP.bitwise_and)
+    cp(A("ICOL"), A("PI", 1, 2))
+    ts(A("C4K"), A("ICOL"), 4096.0, OP.mult)
+    ts(A("LMASK"), A("RI"), A("ICOL"), OP.is_equal)
+    cp(A("BCL"), A("BCI", 0, 8))
+    cp(A("BCS"), A("BCI", 8, 16))
+    cp(A("WF"), A("WI"))
+    ts(A("W8"), A("R8"), 1.0 / 65536, OP.mult, A("WF"), OP.mult)
+    for h in ("_1", "_0"):
+        for nm in ("SC2", "NR", "Y", "FV", "KM0", "KM1", "KM2"):
+            fill(A(nm + h), 0.0)
+        fill(A("ND" + h), 0)
+        for l in "0123":
+            fill(A("ST" + l + h), 0.0)
+            fill(A("ST" + l + h, 0, 112, 1, (32, 34)), 1.0)
+    fill(A("SI"), 0)
+    fill(A("H"), 0)
+    cp(A("H", 0, 128, 8), A("ONF", 0, 16))
+    for nm in ("NB", "DST", "PM_", "S0", "FAR", "CAN", "DMIN"):
+        fill(A(nm), 0.0)
+    fill(A("PT", M, W), 0.0)
+    fill(A("CHI", M, CW), 0)
+    cp(A("R0F"), A("R0I"))
+    for h in (1, 0):
+        for t in range(VI):
+            a = t * L + K0[h]
+            mm(A("FB%d" % h, 8 * t, 8 * t + 8, 1, (0, NL[h])), A("R0F", a, a + NL[h]), A("IF", 0, 8, 1, (0, 8)))
+        ts(A("R0S_%d" % h, 0, 24, 1, (0, NL[h])), A("FB%d" % h, 0, 24, 1, (0, NL[h])), 65536.0, OP.mult)
+    ts(A("IN"), A("IB"), -1.0, OP.mult)
+    ts(A("I25"), A("IB"), 33554432.0, OP.mult)
+    fill(A("TRP"), 8192.0)
+    for nm in ("B5", "MW", "SELA"):
+        fill(A(nm), 0.0)
+    fill(A("MI"), 0)
+    cp(A("MI", 4, 256, 16), A("ONF", 0, 16))
+    fill(A("MCI"), 0)
+    for t in (0, 1):
+        fill(A("SEND%d" % t, 208, 368), -1.0)
+        fill(A("SEND%d" % t, 576, 736), 0.0)
+        ts(A("QF1", t * L, t * L + L), A("QA", (t + 1) * L, (t + 2) * L), 1.0, OP.add)
+        cp(A("QC%d" % (t + 1), CAP, L), A("QA", (t + 1) * L + CAP, (t + 2) * L))
+    cp(A("THF"), A("THI"))
+    ts(A("THB"), A("ONB"), A("THF"), OP.mult)
+    asel(A("TRI"), A("ONB"), [[1, 128]], OP.is_ge, 0.0, -1, -1)
+    asel(A("TRP", 0, 112), A("TRP", 0, 112), [[1, 112]], OP.is_ge, 0.0, 0, -1)
+    asel(A("TRP", 112, 320), A("TRP", 112, 320), [[1, 208]], OP.is_ge, 0.0, -112, -1)
+    asel(A("B5"), A("B5"), [[-16, 8], [0, 16]], OP.not_equal, 1.0, -5, 1)
+    for c, j, v in ((0, 0, 65536.0), (8, 1, 1.0), (8, 2, 64.0), (8, 3, 4096.0), (16, 4, 1.0)):
+        asel(A("MW", c, c + 8), A("MW", c, c + 8), [[-16, 8]], OP.not_equal, v, -j, 1)
+    iota(A("KC"), [[112, 2], [0, 8]], 0, 1, True)
+    iota(A("KJ"), [[112, 2], [0, 8]], W, 1, True)
+    iota(A("KN"), [[1, L]], M, 0, True)
+    for j, v in ((1, 1.0), (2, 64.0)):
+        asel(A("SELA"), A("SELA"), [[-16, 8], [0, L]], OP.not_equal, v, -j, 1)
+    mm(A("FB1", 64, 72), A("THB"), A("R8"))
+    ts(A("TH"), A("FB1", 64, 72), 1.0 / 16, OP.mult)
+
+    def RW(nm, h, c0=0, c1=None, st=1):
+        return A(nm + str(h) if nm + str(h) in PSUMS else nm + "_" + str(h), c0, c1, st, (0, NL[h]))
+
+    HB = lambda nm, h, c0=0, c1=None, st=1: A(nm + "_" + str(h), c0, c1, st)
+    SI = lambda h, a, b: A("SI", 16 * h + a, 16 * h + b, 1, (0, NL[h]))
+    LAST = lambda nm, h: RW(nm, h, 15, 128, 16)
+    SEG = lambda h: A("SEGR", 0, 128, 1, (0, NL[h]))
+    EYE = lambda nm, k: A(nm, 0, k, 1, (0, k))
+    hc = lambda nm, h, r=None: A(nm, 8 * h, 8 * h + 8, 1, (0, NL[h] if r is None else r))
+
+    def to_list(win, h):
+        tt(HB("LB", h), ind(win, A("BCL")), A("LMASK"), OP.mult)
+        mm(A("KEY%d" % h, 128, 128 + NL[h] // 16), RW("LB", h), A("CMASK", 0, NL[h] // 16, 1, (0, NL[h])))
+
+    def list_copy(out, h):
+        cp(out, A("KEY%d" % h, 128, 128 + NL[h] // 16))
+
+    def kids(h):
+        k = NL[h] // 16
+        list_copy(HB("LT", h, 0, k), h)
+        act(HB("PF", h, 0, NL[h]), ind(A("CH"), HB("LT", h, 0, k)), AF.Copy)
+
+    def kids_copy(h):
+        ts(HB("P16", h, 0, NL[h]), HB("PF", h, 0, NL[h]), A("C4K"), OP.subtract)
+
+    def masks(h, lev, want_y, fbs):
+        nl = NL[h]
+        stt = lambda l, k=34: A("ST%d_%d" % (min(l, 3), h), 0, nl, 1, (0, k))
+        mm(A("ZB%d" % h, 384, 384 + nl, 1, (0, 16)), RW("ST", h), EYE("IB", nl))
+        act(stt(lev, 16), A("ZB%d" % h, 384, 384 + nl, 1, (0, 16)), AF.Copy)
+        mm(RW("ZB", h, 0, 384), stt(lev), A("ZC", 0, 384, 1, (0, 34)))
+        act(RW("U", h), RW("ZB", h, 128, 384), AF.Relu, float(TOP))
+        if want_y:
+            act(RW("Y", h), RW("ZB", h, 0, 128), AF.Abs, float(TOP))
+        for c, u, l, k, es in fbs:
+            mm(RW("FB", h, 128, 384), stt(l), A("ZC", 384, 640, 1, (0, 34)), True, False)
+            mm(RW("FB", h, 128, 384), stt(lev), A("ZC", 640, 896, 1, (0, 34)), False, True)
+            act(RW(u, h), RW("FB", h, 128, 384), AF.Relu, float(TOP))
+
+    def fallback(h, fbs):
+        for c, u, l, k, es in fbs:
+            o = RW("FB", h, c, c + 128)
+            mm(o, EYE("IF", NL[h]), RW(k, h), True, False)
+            for e in es:
+                mm(o, EYE("I25", NL[h]), RW(e, h), False, False)
+            mm(o, EYE("IB", NL[h]), RW(u, h, 0, 128), False, False)
+            mm(o, EYE("IB", NL[h]), RW(u, h, 128, 256), False, True)
+
+    def points_scalar(h, a, b):
+        z = turn[0] = 1 - turn[0]
+        w = 16 * (b - a)
+        x, o = A("XG%d" % z, 0, w), A("SP%d" % z, 0, w)
+        act(x, ind(A("PT"), HB("P16", h, a, b)), AF.Copy)
+        mm(o, A("IN"), A("Q16", 16 * (K0[h] + a), 16 * (K0[h] + b)), True, False)
+        mm(o, A("IB"), x, False, True)
+        act(HB("DT", h, 16 * a, 16 * b), o, AF.Abs)
+
+    def points_vector(h, a, b):
+        d = HB("DT", h, 16 * a, 16 * b)
+        tt(d, ind(A("PT"), HB("P16", h, a, b)), A("Q16", 16 * (K0[h] + a), 16 * (K0[h] + b)), OP.subtract)
+        act(d, d, AF.Abs)
+
+    def points(h):
+        for (a, b), (c, d) in zip(VS[h], SS[h]):
+            points_scalar(h, c, d)
+            points_vector(h, a, b)
+
+    def keys(h):
+        nl = NL[h]
+        o = RW("KEY", h, 0, 128)
+        mm(o, HB("PF", h, 0, nl), A("IF"), True, False)
+        mm(o, EYE("IB", nl), RW("U", h, 0, 128), False, False)
+        mm(o, EYE("IB", nl), RW("U", h, 128, 256), False, False)
+        for i in range(16):
+            mm(RW("KEY", h, i, 128, 16), HB("DT", h, i, 16 * nl, 16), A("R8"), False, i == 15)
+
+    FBS = {2: [(0, "UF", 0, "KM0", ("EA",))], 3: [(0, "UF", 1, "KM1", ("EB",))],
+           4: [(0, "UF", 2, "KM2", ("EC",)), (384, "UG", 0, "KM0", ("EA", "ED"))]}
+
+    def look(h, s):
+        scan(RW("SC1", h), SEG(h), RW("KEY", h, 0, 128), OP.max, OP.min)
+        t1, rho = A("H", h * 64 + s + 1, h * 64 + 64, 8, (0, NL[h])), SI(h, 8, 16)
+        tt(t1, LAST("SC1", h), RW("RBC", h) if s == 1 else rho, OP.min)
+        ts(rho, t1, 16711680, OP.bitwise_and)
+        if s == ST + 1:
+            return
+        ts(RW("NR", h), rho, -256.0, OP.mult, -7.5 * TOP, OP.add)
+        tt(HB("X", h), ind(HB("NR", h), A("BCL")), HB("Y", h), OP.add)
+        km = "KM%d" % min(s - 1, 3)
+        tt(RW(km, h), RW("KEY", h, 0, 128), RW("X", h), OP.max)
+        scan(RW("SC2", h), SEG(h), RW(km, h), OP.max, OP.min)
+        if s >= 3:
+            scan(RW("FS", h), SEG(h), RW("FB", h, 0, 128), OP.max, OP.min)
+            if s == 5:
+                scan(RW("FS2", h), SEG(h), RW("FB", h, 384, 512), OP.max, OP.min)
+            ts(RW("FC", h), LAST("FS2" if s == 5 else "FS", h), float(TOP), OP.min)
+            if s == 5:
+                tt(RW("FX", h), RW("PA", h), RW("PB", h), OP.min)
+                tt(RW("FX", h), RW("FX", h), RW("FC", h), OP.max)
+                tt(RW("FC", h), RW("FX", h), LAST("FS", h), OP.min)
+            tt(RW("FV", h), RW("FC", h), RW({3: "PA", 4: "PB", 5: "PC"}[s], h), OP.max)
+            tt(RW("SEL", h), LAST("SC2", h), RW("FV", h), OP.min)
+        else:
+            ts(RW("SEL", h), LAST("SC2", h), float(TOP), OP.min)
+        ts(RW("ND", h), RW("SEL", h), 4095, OP.bitwise_and)
+        to_list(HB("ND", h), h)
+        ts(SI(h, 0, 8), RW("SEL", h), 33488896, OP.bitwise_and)
+        ts(RW("ST", h), SI(h, 0, 16), 1.0 / 65536, OP.mult)
+        masks(h, s, s < ST, FBS.get(s, []))
+        if s in (2, 3, 4):
+            ts(RW({2: "PA", 3: "PB", 4: "PC"}[s], h), RW("SEL", h), TOP, OP.is_lt, float(TOP), OP.mult)
+        if s <= 3:
+            tt(HB({1: "EA", 2: "EB", 3: "EC"}[s], h), ind(HB("SC2", h), A("BCS")), HB(km, h), OP.is_equal)
+        if s == 3:
+            tt(HB("ED", h), ind(HB("FV", h), A("BCL")), HB("KM0", h), OP.is_equal)
+
+    QN = ("QA", "QC1", "QC2")
+    nh = (112, CAP - 112)
+    for t in range(VI):
+        q = lambda a, b: A(QN[t], a, b)
+        if t:
+            ld = "LAND%d" % (t - 1)
+            op("x", None, [], [A(ld)], "x", T.sem["arr%d" % (t - 1)], 8)
+            ts(A("FM"), A(ld, 0, CAP), 0.0, OP.is_lt)
+            tt(A("FQ"), A("FM"), A("QF1", (t - 1) * L, (t - 1) * L + CAP), OP.mult)
+            tt(q(0, CAP), A("FQ"), A(ld, 0, CAP), OP.add)
+        for h in (1, 0):
+            mm(RW("KEY", h, 136, 144), q(K0[h], K0[h] + NL[h]), A("W8"))
+            if t:
+                mm(A("KEY%d" % h, 152, 176, 1, (0, nh[h])), A(ld, CAP + K0[h], CAP + K0[h] + nh[h]), A("MW"))
+        for h in (1, 0):
+            cp(RW("SEL", h), RW("KEY", h, 136, 144))
+            ts(RW("ND", h), RW("SEL", h), 63, OP.bitwise_and)
+            ts(RW("ND", h), RW("ND", h), 1, OP.add)
+            to_list(HB("ND", h), h)
+        for i in range(16):
+            if i < 10:
+                cp(A("Q16", i, 16 * L, 16), q(0, L))
+            else:
+                act(A("Q16", i, 16 * L, 16), q(0, L), AF.Copy)
+        for h in (1, 0):
+            cp(SI(h, 8, 16), RW("R0S", h, 8 * t, 8 * t + 8))
+            if t:
+                r = (0, nh[h])
+                k = lambda a: A("KEY%d" % h, a, a + 8, 1, r)
+                nf = hc("NF", h, nh[h])
+                ts(nf, k(168), 0.0, OP.is_equal)
+                tt(nf, nf, A("R0S_%d" % h, 8 * t, 8 * t + 8, 1, r), OP.mult)
+                tt(A("SI", 16 * h + 8, 16 * h + 16, 1, r), k(152), nf, OP.add)
+                ts(hc("NB", h, nh[h]), k(160), -1.0, OP.mult)
+        if t == 0:
+            for a, b in ((0, 1152), (1152, CW)):
+                ts(A("CH", a, b), A("CHI", a, b), A("C4K"), OP.add)
+            fill(A("PT", 0, 1), 256.0)
+        for h in (1, 0):
+            k = NL[h] // 16
+            kids(h)
+            a0 = HB("A0", h, 0, NL[h])
+            tt(a0, ind(A("PT"), HB("LT", h, 0, k)), q(K0[h], K0[h] + NL[h]), OP.subtract)
+            act(a0, a0, AF.Abs)
+            mm(RW("KEY", h, 144, 152), a0, A("R8"))
+            kids_copy(h)
+        for h in (1, 0):
+            cp(SI(h, 0, 8), RW("KEY", h, 144, 152))
+            ts(RW("ST", h), SI(h, 0, 16), 1.0 / 65536, OP.mult)
+            masks(h, 0, True, [])
+            tt(RW("SEL", h), SI(h, 0, 8), SI(h, 8, 16), OP.is_lt)
+            tt(RW("RBC", h), SI(h, 0, 8), SI(h, 8, 16), OP.min)
+            tt(A("H", h * 64 + 1, h * 64 + 64, 8, (0, NL[h])), RW("SEL", h), RW("ND", h), OP.mult)
+        for h in (1, 0):
+            points(h)
+            keys(h)
+        for s in range(1, ST + 2):
+            for h in (1, 0):
+                half[0] = h
+                look(h, s)
+            if s <= ST:
+                for h in (1, 0):
+                    half[0] = h
+                    kids(h)
+                    kids_copy(h)
+                    points(h)
+                    keys(h)
+                    fallback(h, FBS.get(s, []))
+        half[0] = 0
+
+        last = t == VI - 1
+        both = lambda nm: A(nm, 0, 16)
+        if not last:
+            for h in (1, 0):
+                tt(hc("FAR", h), SI(h, 8, 16), A("TH", 0, 8, 1, (0, NL[h])), OP.is_ge)
+            mm(RW("FB", 0, 0, 8), EYE("TRI", 112), hc("FAR", 0))
+            mm(RW("FB", 1, 0, 8), EYE("TRI", 96), hc("FAR", 1), True, False)
+            mm(RW("FB", 1, 0, 8), A("ONB", 0, 96, 1, (0, 112)), hc("FAR", 0), False, True)
+            for h in (1, 0):
+                ts(hc("PM_", h), RW("FB", h, 0, 8), float(CAP), OP.min)
+                ts(hc("S0", h), RW("FB", h, 0, 8), float(CAP), OP.is_lt)
+            tt(both("DA"), both("KC"), both("PM_"), OP.subtract)
+            tt(both("S0"), both("S0"), both("FAR"), OP.mult)
+            tt(both("DB"), both("PM_"), both("DA"), OP.subtract)
+            ts(both("DB"), both("DB"), 208.0, OP.add)
+            tt(both("DB"), both("DB"), both("S0"), OP.mult)
+            tt(both("DST"), both("DA"), both("DB"), OP.add)
+            for h in (1, 0):
+                to_list(A("DST", 8 * h, 8 * h + 8), h)
+        ts(A("LW"), A("H"), 4095, OP.bitwise_and)
+        ts(A("LD0"), A("LW"), 0, OP.is_equal)
+        cp(A("LF"), A("LW"))
+        cp(A("LF", 0, 128, 8), both("NB"))
+        scan(A("LS"), A("LD0"), A("LF"), OP.mult, OP.add)
+        res = A("LS", 7, 128, 8)
+        ts(both("NOD"), res, 0.0, OP.max)
+        ts(both("E1"), res, 0.0, OP.is_gt, 4096.0 * rank, OP.mult)
+        tt(both("BST"), both("NOD"), both("NOD"), OP.add)
+        tt(both("E1"), both("E1"), res, OP.subtract)
+        tt(both("BST"), both("BST"), both("E1"), OP.add)
+        if not last:
+            for h in (1, 0):
+                list_copy(A("DL", 7 * h, 7 * h + NL[h] // 16), h)
+            w1, w2 = (ind(A("SEND%d" % t, a, a + 368), A("DL", 0, 13)) for a in (0, 368))
+            cp(w1, q(0, L))
+            for h in (1, 0):
+                for j, k in ((0, 16), (5, 20)):
+                    ts(A("MI", 128 * h + j, 128 * h + 128, 16, (0, NL[h])), SI(h, 8, 16), k, OP.logical_shift_right)
+            cp(both("BEST"), both("BST"))
+            ts(A("MI", 1, 256, 16), both("BEST"), 63, OP.bitwise_and)
+            ts(A("MI", 2, 256, 16), both("BEST"), 6, OP.logical_shift_right, 63, OP.bitwise_and)
+            ts(A("MI", 3, 256, 16), both("BEST"), 12, OP.logical_shift_right)
+            cp(A("ML"), A("MI"))
+
+            def to_gp():
+                for h in (1, 0):
+                    mm(A("ZB0", K0[h], K0[h] + NL[h]), A("ML", 128 * h, 128 * h + 128, 1, (0, NL[h])), EYE("IB", NL[h]))
+            to_gp()
+            act(A("MG"), A("ZB0", 0, L), AF.Copy)
+            cp(w2, A("MG"))
+            dst = cores[(rank + 1) % n]
+            hop = hop_of(core, dst, cores, topo)
+            rid, pid = topo.addr(hop, core)
+            m = some(topo.engines(core, hop), 4)
+            tr = [RemoteDMATransfer(dst_ids=[DstId(rid=rid, pnc=pid)], dma_engine_mask=m[i], remote_sem=T.sem["arr%d" % t],
+                                    src=T["SEND%d" % t][:, a:a + CAP], dst=T["LAND%d" % t][:, i * CAP:(i + 1) * CAP])
+                  for i, a in ((0, 208), (1, 576))]
+            op("g", lambda tr=tr, t=t: g.remote_dma_fused(tr, local_sem=T.sem["loc%d" % t]), [A("SEND%d" % t)], [], "r",
+               T.sem["loc%d" % t], 8, 1.0)
+        for h in (1, 0):
+            ts(A("OUTL", 16 * h, 16 * h + 8, 1, (0, NL[h])), SI(h, 8, 16), 1.0 / 65536, OP.mult)
+            cp(A("OUTL", 16 * h + 8, 16 * h + 16, 1, (0, NL[h])), hc("BST", h))
+            mm(A("ZB1", K0[h], K0[h] + NL[h], 1, (0, 16)), A("OUTL", 16 * h, 16 * h + 16, 1, (0, NL[h])), EYE("IF", NL[h]))
+        yo = A("YO", t * L, t * L + L)
+        act(yo, A("ZB1", 0, L, 1, (0, 16)), AF.Copy)
+        dma("y", T.yr[:, t * L:t * L + L], A("YO", t * L, t * L + L, 1, (0, 8))[0], [yo], [])
+        dma("y", T.yb[:, t * L:t * L + L], A("YO", t * L, t * L + L, 1, (8, 16))[0], [yo], [])
+        if last:
+            break
+        for h in (1, 0):
+            to_list(A("NOD", 8 * h, 8 * h + 8), h)
+        cp(A("PT", M + t * L, M + t * L + L), q(0, L))
+        for h in (1, 0):
+            list_copy(A("NLT", 7 * h, 7 * h + NL[h] // 16), h)
+        act(A("GG"), ind(A("CH"), A("NLT", 0, 13)), AF.Copy)
+        mm(A("ZB0", 256, 256 + L), A("B5"), A("MG"))
+        ts(A("OB"), A("ZB0", 256, 256 + L), A("ICOL"), OP.is_equal)
+        ts(A("BN"), A("KN"), float(t * L), OP.add)
+        tt(A("BN"), A("BN"), A("OB"), OP.mult)
+        ts(A("EE"), A("GG"), A("C4K"), OP.is_equal)
+        tt(A("EE"), A("EE"), A("OB"), OP.mult)
+        for h in (1, 0):
+            mm(RW("SP", h, 0, 8), A("EE", K0[h], K0[h] + NL[h]), A("R8"))
+        tt(both("YPL"), both("FAR"), both("NOD"), OP.mult)
+        for h in (1, 0):
+            ts(hc("CAN", h), RW("SP", h, 0, 8), 1.0 / 65536, OP.mult)
+        tt(both("YPL"), both("YPL"), both("CAN"), OP.mult)
+        cp(both("NCI"), both("YPL"))
+        ts(A("MCI", 1, 256, 16), both("NCI"), 63, OP.bitwise_and)
+        ts(A("MCI", 2, 256, 16), both("NCI"), 6, OP.logical_shift_right)
+        cp(A("ML"), A("MCI"))
+        to_gp()
+        act(A("MG"), A("ZB0", 0, L), AF.Copy)
+        act(A("MGN"), A("ZB0", 0, L), AF.Copy, -1.0)
+        banks, z = ("FB0", "FB1", "ZB0", "ZB1"), 0
+        for gr in range(8):
+            for h in (1, 0):
+                nl, w = NL[h], K0[h] + NL[h]
+                o = A(banks[z % 4], 0, w, 1, (0, nl))
+                z += 1
+                mm(o, A("SELA", gr * L, gr * L + nl), A("MG", 0, w), True, False)
+                mm(o, A("MGN", K0[h], K0[h] + nl), A("SELA", gr * L, gr * L + w), False, False)
+                mm(o, EYE("IB", nl), A("TRP", 112 * h, 112 * h + w, 1, (0, nl)), False, True)
+                least(A("DMIN", 8 * h + gr, 8 * h + gr + 1, 1, (0, nl)), o)
+        ts(both("DMIN"), both("DMIN"), 0.0, OP.is_gt)
+        tt(both("YPL"), both("YPL"), both("DMIN"), OP.mult)
+        ts(both("DA"), both("YPL"), 0.0, OP.is_equal)
+        tt(both("DA"), both("DA"), both("KJ"), OP.mult)
+        tt(both("DST"), both("DA"), both("YPL"), OP.add)
+        for h in (1, 0):
+            to_list(A("DST", 8 * h, 8 * h + 8), h)
+        for h in (1, 0):
+            list_copy(A("DL2", 7 * h, 7 * h + NL[h] // 16), h)
+        tt(ind(A("CH"), A("DL2", 0, 13)), A("GG"), A("BN"), OP.add)
+        for h in (1, 0):
+            mm(A("ZB1", K0[h], K0[h] + NL[h], 1, (0, 8)), hc("YPL", h), EYE("IF", NL[h]))
+        yo = A("YPO", t * L, t * L + L)
+        act(yo, A("ZB1", 0, L, 1, (0, 8)), AF.Copy)
+        dma("y", T.yp[:, t * L:t * L + L], yo[0], [yo], [])
+
+    if not PLAN:
+        PLAN.update(plan(ops))
+    emit(g, ops, QUE, SEM)
+
+
+def plan(ops):
+    def meets(a, b):
+        if a[2] >= b[3] or b[2] >= a[3] or a[4] >= b[5] or b[4] >= a[5]:
+            return False
+        return not (a[6] == b[6] and a[6] > 1 and (a[4] - b[4]) % a[6] != 0)
+
+    N = len(ops)
+    tag = [o[0] if o[4] == "c" else "a%d" % i for i, o in enumerate(ops)]
+    hist, deps, sent, pool = {}, [], [], []
+    for i in range(N):
+        R, Wr, kind, dep = ops[i][2], ops[i][3], ops[i][4], set()
+        for lst, w in ((R, False), (Wr, True)):
+            for r in lst:
+                ps = r[1] in PSUMS
+                for (j, rr, ww) in hist.get(r[1], []):
+                    if j != i and ((ps and (tag[j] != tag[i] or w or ww)) or ((w or ww) and meets(r, rr))):
+                        dep.add(j)
+        if tag[i] == "g":
+            dep.update(pool[-1:])
+            pool.append(i)
+        if kind == "x":
+            dep.add(sent[-1])
+        if kind == "r":
+            sent.append(i)
+        deps.append(dep)
+        for lst, w in ((R, False), (Wr, True)):
+            for r in lst:
+                h = hist.setdefault(r[1], [])
+                if w and r[1] in PSUMS:
+                    h[:] = []
+                elif w and r[6] == 1:
+                    h[:] = [e for e in h if not (r[2] <= e[1][2] and e[1][3] <= r[3] and r[4] <= e[1][4] and e[1][5] <= r[5])]
+                h.append((i, r, w))
+    after = [{"c": 0.06, "d": 2.2, "r": 7.5, "x": 0.1}[o[4]] for o in ops]
+    nxt = [[] for _ in range(N)]
+    for i in range(N):
+        for j in deps[i]:
+            nxt[j].append((i, tag[i] == tag[j] == "t"))
+    way = [0.0] * N
+    for i in range(N - 1, -1, -1):
+        way[i] = ops[i][7] + after[i] + max([way[k] for k, st in nxt[i]] or [0.0])
+    best = None
+    for bias, noise, hold, seed in TRIES:
+        order, when, end = in_time(ops, deps, nxt, after, way, bias, noise, hold, seed)
+        if best is None or end < best[0]:
+            best = (end, order, when)
+    order, when = best[1], best[2]
+    seq, num = {q: 0 for q in "vstg"}, [1] * N
+    known = {q: {} for q in "vstgyx"}
+    snap, need, waits = [None] * N, set(), [None] * N
+    for i in order:
+        q = ops[i][0]
+        if ops[i][4] == "c":
+            seq[q] += 1
+            num[i] = seq[q]
+        k, mine, last = known[q], [], {}
+        for j in deps[i]:
+            if ops[i][4] == "x" or tag[j] == tag[i] == "t":
+                continue
+            if tag[j] not in last or num[last[tag[j]]] < num[j]:
+                last[tag[j]] = j
+        for j in sorted(last.values(), key=lambda j: -when[j]):
+            if k.get(tag[j], 0) >= num[j]:
+                continue
+            mine.append(j)
+            need.add(j)
+            for a, b in snap[j].items():
+                if k.get(a, 0) < b:
+                    k[a] = b
+        waits[i] = mine
+        snap[i] = dict(k)
+        snap[i][tag[i]] = num[i]
+    return {"order": order, "waits": waits, "need": need}
+
+
+def in_time(ops, deps, nxt, after, way, bias, noise, hold, seed):
+    N = len(ops)
+    left = [len(d) for d in deps]
+    when = [0.0] * N
+    free = {q: 0.0 for q in "vstgyx"}
+    ready = {q: [i for i in range(N) if ops[i][0] == q and left[i] == 0] for q in free}
+    z, pr = seed, []
+    for i in range(N):
+        z = (1103515245 * z + 12345) % 2147483648
+        pr.append(way[i] + bias * ops[i][8] + noise * z / 2147483648.0)
+    order = []
+    while len(order) < N:
+        best = None
+        for q in free:
+            if ready[q]:
+                t = max(free[q], min(when[i] for i in ready[q]))
+                if best is None or t < best[0]:
+                    best = (t, q)
+        t, q = best
+        i = max((i for i in ready[q] if when[i] <= t + hold), key=lambda k: (pr[k], -k))
+        ready[q].remove(i)
+        free[q] = max(t, when[i]) + ops[i][7]
+        end = free[q] + after[i]
+        order.append(i)
+        for k, st in nxt[i]:
+            left[k] -= 1
+            when[k] = max(when[k], free[q] if st else end)
+            if left[k] == 0:
+                ready[ops[k][0]].append(k)
+    return order, when, max(free.values())
+
+
+def emit(g, ops, QUE, SEM):
+    cnt, at = {q: 0 for q in "vstg"}, {}
+    for i in PLAN["order"]:
+        q, fn, R, Wr, kind, sem, val = ops[i][:7]
+        if kind == "x":
+            continue
+        for j in PLAN["waits"][i]:
+            s, v = at[j] if j in at else (ops[j][5], ops[j][6])
+            QUE[q].wait_ge(s, v)
+        inst = fn()
+        if kind == "d":
+            inst.then_inc(sem, val)
+        elif kind == "c" and i in PLAN["need"]:
+            cnt[q] += 1
+            inst.then_inc(SEM[q], 1)
+            at[i] = (SEM[q], cnt[q])
+    for q in cnt:
+        if cnt[q]:
+            g.wait_ge(SEM[q], cnt[q])
+    for o in ops:
+        if o[4] in ("d", "r", "x"):
+            g.wait_ge(o[5], o[6])

@@ -6,7 +6,7 @@ W = M + (VI - 1) * L
 CW = W + L
 NL, K0 = (112, 96), (0, 112)
 TOP = 16777216
-CYC = 0.00083
+CYC = 0.00104
 VS = {0: ((0, 28), (28, 56)), 1: ((0, 24), (24, 48))}
 SS = {0: ((56, 84), (84, 112)), 1: ((48, 72), (72, 96))}
 TRIES = [(0.3 * b, 0.3 * (s > 1), 1e-9, s) for b in range(12) for s in range(1, 12)]
@@ -37,13 +37,14 @@ def _pool(dtype, halves, **bufs):
 
 
 _pool("bfloat16", dict(DT=1792, A0=112, ST=16, ST0=112, ST1=112, ST2=112, ST3=112, U=256, UF=256, UG=256, EA=128, EB=128, EC=128,
-                       ED=128), THB=128, ONB=128, IB=128, I25=128, IN=128, R8=8, W8=8, ZC=896, TRI=128, TRP=320, B5=128, MW=24,
-      SELA=8 * L, FAR=16, ML=256, MG=L, MGN=L, EE=L, FM=CAP, FQ=CAP, QF1=2 * L, XG0=512, XG1=512, QC1=L, QC2=L)
+                       ED=128), THB=128, ONB=128, IB=128, I25=128, IN=128, R8=8, W8=8, ZC=896, TRI=128, TRP=112, B5=128, MW=24,
+      LG=4 * L, FAR=16, ML=256, ML2=256, MG=L, MGN=L, EE=L, FM=CAP, FQ=CAP, QF1=2 * L, XG0=512, XG1=512, QC1=L, QC2=L)
 _pool("float32", dict(PF=112, SC1=128, SC2=128, FS=128, FS2=128, NR=8, X=128, Y=128, LB=128, FC=8, FV=8, FX=8, R0S=24, KM0=128,
                       KM1=128, KM2=128, KM3=128, PA=8, PB=8, PC=8), WF=1, THF=1, ONF=128, IF=128, ICOL=1, C4K=1, LMASK=128,
-      CMASK=8, SEGR=128, KC=16, KJ=16, KN=L, TH=8, LD0=128, LF=128, LS=128, NB=16, PM_=16, S0=16, DA=16, DB=16, DST=16, NOD=16,
-      E1=16, BST=16, OUTL=32, GG=L, OB=L, BN=L, CAN=16, DMIN=16, YPL=16, NF=16)
-_pool("int32", dict(SEL=8, ND=8, RBC=8), PI=2, RI=128, BCI=16, H=128, LW=128, SI=32, BEST=16, MI=256, MCI=256, NCI=16)
+      CMASK=8, SEGR=128, KC=16, KC2=16, KJ=16, KN=L, TH=8, LD0=128, LF=128, LS=128, NB=16, S0=16, DA=16, DB=16, DST=16,
+      NOD=16, Z1=16, N1=16, B1=16, GMF=8, BST=16, OUTL=32, GG=L, OB=L, BN=L, CAN=16, DMIN=16, YPL=16, NF=16)
+_pool("int32", dict(SEL=8, ND=8, RBC=8), PI=2, RI=128, BCI=16, H=128, LW=128, LWL=16, SI=32, BEST=16, MI=256, MCI=256, MCJ=256,
+      NCI=16)
 _pool("uint16", dict(P16=112, LT=8), BCL=8, BCS=8, DL=14, NLT=14, DL2=14)
 SEMAPHORES = ["cv", "cs", "ct", "cg", "arr0", "arr1", "loc0", "loc1"] + ["d%d" % i for i in range(16)]
 PLAN = {}
@@ -117,7 +118,7 @@ def rank_program(g, core, T, topo):
         if q == "s":
             return 0.065 + m * (1.5 if is_ind(ins[0]) else 1) * CYC
         if q == "t":
-            return max(min(64, size(ins[0])), m) * 0.0005 * (4 if SIZES[ins[0][1]][1] == "float32" else 1)
+            return max(min(64, size(ins[0])), m) * 0.0007 * (4 if SIZES[ins[0][1]][1] == "float32" else 1)
         return 0.15 + 2 * m * CYC
 
     def op(q, fn, rd, wr, kind="c", sem=None, val=1, c=0.1):
@@ -209,7 +210,7 @@ def rank_program(g, core, T, topo):
         iota(z, [[0, 8], [sgn, 16]], 0, 0, True)
         asel(z, z, [[0, 128]], OP.not_equal, c, -1, 1)
     cp(A("ZC", 640, 896, 1, (32, 34)), A("ZC", 128, 384, 1, (32, 34)))
-    asel(A("SEGR"), A("SEGR"), [[0, 8], [1, 16]], OP.not_equal, 2147483648.0, 0, 0)
+    asel(A("SEGR"), A("SEGR"), [[0, 8], [1, 16]], OP.not_equal, float(TOP), 0, 0)
     ts(A("PI", 1, 2), A("PI", 0, 1), 15, OP.bitwise_and)
     cp(A("ICOL"), A("PI", 1, 2))
     ts(A("C4K"), A("ICOL"), 4096.0, OP.mult)
@@ -228,7 +229,7 @@ def rank_program(g, core, T, topo):
     fill(A("SI"), 0)
     fill(A("H"), 0)
     cp(A("H", 0, 128, 8), A("ONF", 0, 16))
-    for nm in ("NB", "DST", "PM_", "S0", "FAR", "CAN", "DMIN"):
+    for nm in ("NB", "DST", "S0", "DB", "FAR", "CAN", "DMIN"):
         fill(A(nm), 0.0)
     fill(A("PT", M, W), 0.0)
     fill(A("CHI", M, CW), 0)
@@ -241,11 +242,14 @@ def rank_program(g, core, T, topo):
     ts(A("IN"), A("IB"), -1.0, OP.mult)
     ts(A("I25"), A("IB"), 33554432.0, OP.mult)
     fill(A("TRP"), 8192.0)
-    for nm in ("B5", "MW", "SELA"):
+    for nm in ("B5", "MW"):
         fill(A(nm), 0.0)
-    fill(A("MI"), 0)
+    for nm in ("MI", "MCI", "MCJ"):
+        fill(A(nm), 0)
     cp(A("MI", 4, 256, 16), A("ONF", 0, 16))
-    fill(A("MCI"), 0)
+    for nm, j, v in (("MCI", 3, -1.0), ("MCI", 4, -64.0), ("MCJ", 1, 1.0), ("MCJ", 2, 64.0)):
+        ts(A(nm, j, 256, 16), A("ONF", 0, 16), v, OP.mult)
+    ts(A("GMF"), A("R8"), 1.0 / 65536, OP.mult)
     for t in (0, 1):
         fill(A("SEND%d" % t, 208, 368), -1.0)
         fill(A("SEND%d" % t, 576, 736), 0.0)
@@ -254,16 +258,15 @@ def rank_program(g, core, T, topo):
     cp(A("THF"), A("THI"))
     ts(A("THB"), A("ONB"), A("THF"), OP.mult)
     asel(A("TRI"), A("ONB"), [[1, 128]], OP.is_ge, 0.0, -1, -1)
-    asel(A("TRP", 0, 112), A("TRP", 0, 112), [[1, 112]], OP.is_ge, 0.0, 0, -1)
-    asel(A("TRP", 112, 320), A("TRP", 112, 320), [[1, 208]], OP.is_ge, 0.0, -112, -1)
+    asel(A("TRI"), A("TRI"), [[1, 128]], OP.not_equal, -512.0, 0, -1)
+    asel(A("TRP"), A("TRP"), [[1, 112]], OP.is_ge, 0.0, 0, -1)
     asel(A("B5"), A("B5"), [[-16, 8], [0, 16]], OP.not_equal, 1.0, -5, 1)
     for c, j, v in ((0, 0, 65536.0), (8, 1, 1.0), (8, 2, 64.0), (8, 3, 4096.0), (16, 4, 1.0)):
         asel(A("MW", c, c + 8), A("MW", c, c + 8), [[-16, 8]], OP.not_equal, v, -j, 1)
     iota(A("KC"), [[112, 2], [0, 8]], 0, 1, True)
+    iota(A("KC2"), [[-112, 2], [0, 8]], 720, -1, True)
     iota(A("KJ"), [[112, 2], [0, 8]], W, 1, True)
     iota(A("KN"), [[1, L]], M, 0, True)
-    for j, v in ((1, 1.0), (2, 64.0)):
-        asel(A("SELA"), A("SELA"), [[-16, 8], [0, L]], OP.not_equal, v, -j, 1)
     mm(A("FB1", 64, 72), A("THB"), A("R8"))
     ts(A("TH"), A("FB1", 64, 72), 1.0 / 16, OP.mult)
 
@@ -287,10 +290,8 @@ def rank_program(g, core, T, topo):
     def kids(h):
         k = NL[h] // 16
         list_copy(HB("LT", h, 0, k), h)
+        ts(HB("P16", h, 0, NL[h]), ind(A("CH"), HB("LT", h, 0, k)), A("C4K"), OP.subtract)
         act(HB("PF", h, 0, NL[h]), ind(A("CH"), HB("LT", h, 0, k)), AF.Copy)
-
-    def kids_copy(h):
-        ts(HB("P16", h, 0, NL[h]), HB("PF", h, 0, NL[h]), A("C4K"), OP.subtract)
 
     def masks(h, lev, want_y, fbs):
         nl = NL[h]
@@ -300,7 +301,7 @@ def rank_program(g, core, T, topo):
         mm(RW("ZB", h, 0, 384), stt(lev), A("ZC", 0, 384, 1, (0, 34)))
         act(RW("U", h), RW("ZB", h, 128, 384), AF.Relu, float(TOP))
         if want_y:
-            act(RW("Y", h), RW("ZB", h, 0, 128), AF.Abs, float(TOP))
+            act(RW("Y", h), RW("ZB", h, 0, 128), AF.Abs, 65536.0 * TOP)
         for c, u, l, k, es in fbs:
             mm(RW("FB", h, 128, 384), stt(l), A("ZC", 384, 640, 1, (0, 34)), True, False)
             mm(RW("FB", h, 128, 384), stt(lev), A("ZC", 640, 896, 1, (0, 34)), False, True)
@@ -350,27 +351,28 @@ def rank_program(g, core, T, topo):
         scan(RW("SC1", h), SEG(h), RW("KEY", h, 0, 128), OP.max, OP.min)
         t1, rho = A("H", h * 64 + s + 1, h * 64 + 64, 8, (0, NL[h])), SI(h, 8, 16)
         tt(t1, LAST("SC1", h), RW("RBC", h) if s == 1 else rho, OP.min)
+        if s <= ST:
+            ts(RW("NR", h), t1, -float(TOP), OP.mult, -7.5 * 65536 * TOP, OP.add)
         ts(rho, t1, 16711680, OP.bitwise_and)
         if s == ST + 1:
             return
-        ts(RW("NR", h), rho, -256.0, OP.mult, -7.5 * TOP, OP.add)
         tt(HB("X", h), ind(HB("NR", h), A("BCL")), HB("Y", h), OP.add)
         km = "KM%d" % min(s - 1, 3)
         tt(RW(km, h), RW("KEY", h, 0, 128), RW("X", h), OP.max)
         scan(RW("SC2", h), SEG(h), RW(km, h), OP.max, OP.min)
         if s >= 3:
             scan(RW("FS", h), SEG(h), RW("FB", h, 0, 128), OP.max, OP.min)
+            fc = LAST("FS", h)
             if s == 5:
                 scan(RW("FS2", h), SEG(h), RW("FB", h, 384, 512), OP.max, OP.min)
-            ts(RW("FC", h), LAST("FS2" if s == 5 else "FS", h), float(TOP), OP.min)
-            if s == 5:
                 tt(RW("FX", h), RW("PA", h), RW("PB", h), OP.min)
-                tt(RW("FX", h), RW("FX", h), RW("FC", h), OP.max)
-                tt(RW("FC", h), RW("FX", h), LAST("FS", h), OP.min)
-            tt(RW("FV", h), RW("FC", h), RW({3: "PA", 4: "PB", 5: "PC"}[s], h), OP.max)
+                tt(RW("FX", h), RW("FX", h), LAST("FS2", h), OP.max)
+                tt(RW("FC", h), RW("FX", h), fc, OP.min)
+                fc = RW("FC", h)
+            tt(RW("FV", h), fc, RW({3: "PA", 4: "PB", 5: "PC"}[s], h), OP.max)
             tt(RW("SEL", h), LAST("SC2", h), RW("FV", h), OP.min)
         else:
-            ts(RW("SEL", h), LAST("SC2", h), float(TOP), OP.min)
+            cp(RW("SEL", h), LAST("SC2", h))
         ts(RW("ND", h), RW("SEL", h), 4095, OP.bitwise_and)
         to_list(HB("ND", h), h)
         ts(SI(h, 0, 8), RW("SEL", h), 33488896, OP.bitwise_and)
@@ -428,7 +430,6 @@ def rank_program(g, core, T, topo):
             tt(a0, ind(A("PT"), HB("LT", h, 0, k)), q(K0[h], K0[h] + NL[h]), OP.subtract)
             act(a0, a0, AF.Abs)
             mm(RW("KEY", h, 144, 152), a0, A("R8"))
-            kids_copy(h)
         for h in (1, 0):
             cp(SI(h, 0, 8), RW("KEY", h, 144, 152))
             ts(RW("ST", h), SI(h, 0, 16), 1.0 / 65536, OP.mult)
@@ -447,7 +448,6 @@ def rank_program(g, core, T, topo):
                 for h in (1, 0):
                     half[0] = h
                     kids(h)
-                    kids_copy(h)
                     points(h)
                     keys(h)
                     fallback(h, FBS.get(s, []))
@@ -462,27 +462,31 @@ def rank_program(g, core, T, topo):
             mm(RW("FB", 1, 0, 8), EYE("TRI", 96), hc("FAR", 1), True, False)
             mm(RW("FB", 1, 0, 8), A("ONB", 0, 96, 1, (0, 112)), hc("FAR", 0), False, True)
             for h in (1, 0):
-                ts(hc("PM_", h), RW("FB", h, 0, 8), float(CAP), OP.min)
-                ts(hc("S0", h), RW("FB", h, 0, 8), float(CAP), OP.is_lt)
-            tt(both("DA"), both("KC"), both("PM_"), OP.subtract)
-            tt(both("S0"), both("S0"), both("FAR"), OP.mult)
-            tt(both("DB"), both("PM_"), both("DA"), OP.subtract)
-            ts(both("DB"), both("DB"), 208.0, OP.add)
+                ts(hc("S0", h), RW("FB", h, 0, 8), float(CAP - 512), OP.is_lt)
+                tt(hc("DB", h), RW("FB", h, 0, 8), hc("KC2", h), OP.add)
             tt(both("DB"), both("DB"), both("S0"), OP.mult)
-            tt(both("DST"), both("DA"), both("DB"), OP.add)
+            tt(both("DST"), both("KC"), both("DB"), OP.add)
             for h in (1, 0):
                 to_list(A("DST", 8 * h, 8 * h + 8), h)
+        ts(both("LWL"), A("H", 7, 128, 8), 4095, OP.bitwise_and)
         ts(A("LW"), A("H"), 4095, OP.bitwise_and)
         ts(A("LD0"), A("LW"), 0, OP.is_equal)
         cp(A("LF"), A("LW"))
         cp(A("LF", 0, 128, 8), both("NB"))
         scan(A("LS"), A("LD0"), A("LF"), OP.mult, OP.add)
-        res = A("LS", 7, 128, 8)
-        ts(both("NOD"), res, 0.0, OP.max)
-        ts(both("E1"), res, 0.0, OP.is_gt, 4096.0 * rank, OP.mult)
-        tt(both("BST"), both("NOD"), both("NOD"), OP.add)
-        tt(both("E1"), both("E1"), res, OP.subtract)
-        tt(both("BST"), both("BST"), both("E1"), OP.add)
+        res = A("LS", 6, 128, 8)
+        ts(both("N1"), res, 0.0, OP.max)
+        ts(both("B1"), res, 0.0, OP.is_gt, 4096.0 * rank, OP.mult)
+        tt(both("B1"), both("B1"), both("N1"), OP.add)
+        tt(both("B1"), both("B1"), both("N1"), OP.add)
+        tt(both("B1"), both("B1"), res, OP.subtract)
+        ts(both("Z1"), both("LWL"), 0, OP.is_equal)
+        tt(both("N1"), both("N1"), both("Z1"), OP.mult)
+        tt(both("NOD"), both("N1"), both("LWL"), OP.add)
+        tt(both("B1"), both("B1"), both("Z1"), OP.mult)
+        ts(both("Z1"), both("Z1"), -4096.0 * rank, OP.mult, 4096.0 * rank, OP.add)
+        tt(both("B1"), both("B1"), both("LWL"), OP.add)
+        tt(both("BST"), both("B1"), both("Z1"), OP.add)
         if not last:
             for h in (1, 0):
                 list_copy(A("DL", 7 * h, 7 * h + NL[h] // 16), h)
@@ -497,9 +501,9 @@ def rank_program(g, core, T, topo):
             ts(A("MI", 3, 256, 16), both("BEST"), 12, OP.logical_shift_right)
             cp(A("ML"), A("MI"))
 
-            def to_gp():
+            def to_gp(z="ZB0", ml="ML"):
                 for h in (1, 0):
-                    mm(A("ZB0", K0[h], K0[h] + NL[h]), A("ML", 128 * h, 128 * h + 128, 1, (0, NL[h])), EYE("IB", NL[h]))
+                    mm(A(z, K0[h], K0[h] + NL[h]), A(ml, 128 * h, 128 * h + 128, 1, (0, NL[h])), EYE("IB", NL[h]))
             to_gp()
             act(A("MG"), A("ZB0", 0, L), AF.Copy)
             cp(w2, A("MG"))
@@ -541,21 +545,24 @@ def rank_program(g, core, T, topo):
             ts(hc("CAN", h), RW("SP", h, 0, 8), 1.0 / 65536, OP.mult)
         tt(both("YPL"), both("YPL"), both("CAN"), OP.mult)
         cp(both("NCI"), both("YPL"))
-        ts(A("MCI", 1, 256, 16), both("NCI"), 63, OP.bitwise_and)
-        ts(A("MCI", 2, 256, 16), both("NCI"), 6, OP.logical_shift_right)
-        cp(A("ML"), A("MCI"))
+        for nm, ml, j in (("MCI", "ML", 1), ("MCJ", "ML2", 3)):
+            ts(A(nm, j, 256, 16), both("NCI"), 63, OP.bitwise_and)
+            ts(A(nm, j + 1, 256, 16), both("NCI"), 6, OP.logical_shift_right)
+            cp(A(ml), A(nm))
         to_gp()
+        to_gp("ZB1", "ML2")
         act(A("MG"), A("ZB0", 0, L), AF.Copy)
-        act(A("MGN"), A("ZB0", 0, L), AF.Copy, -1.0)
+        act(A("MGN"), A("ZB1", 0, L), AF.Copy)
         banks, z = ("FB0", "FB1", "ZB0", "ZB1"), 0
         for gr in range(8):
+            lg = gr % 4 * L
+            ts(A("LG", lg, lg + L), A("MGN"), A("GMF", gr, gr + 1), OP.mult)
             for h in (1, 0):
                 nl, w = NL[h], K0[h] + NL[h]
                 o = A(banks[z % 4], 0, w, 1, (0, nl))
                 z += 1
-                mm(o, A("SELA", gr * L, gr * L + nl), A("MG", 0, w), True, False)
-                mm(o, A("MGN", K0[h], K0[h] + nl), A("SELA", gr * L, gr * L + w), False, False)
-                mm(o, EYE("IB", nl), A("TRP", 112 * h, 112 * h + w, 1, (0, nl)), False, True)
+                mm(o, A("LG", lg + K0[h], lg + w), A("MG", 0, w), True, False)
+                mm(A(o[1], K0[h], w, 1, (0, nl)), EYE("IB", nl), A("TRP", 0, nl, 1, (0, nl)), False, True)
                 least(A("DMIN", 8 * h + gr, 8 * h + gr + 1, 1, (0, nl)), o)
         ts(both("DMIN"), both("DMIN"), 0.0, OP.is_gt)
         tt(both("YPL"), both("YPL"), both("DMIN"), OP.mult)
@@ -611,7 +618,7 @@ def plan(ops):
                 elif w and r[6] == 1:
                     h[:] = [e for e in h if not (r[2] <= e[1][2] and e[1][3] <= r[3] and r[4] <= e[1][4] and e[1][5] <= r[5])]
                 h.append((i, r, w))
-    after = [{"c": 0.06, "d": 2.2, "r": 7.5, "x": 0.1}[o[4]] for o in ops]
+    after = [{"c": 0.12, "d": 2.2, "r": 7.5, "x": 0.1}[o[4]] for o in ops]
     nxt = [[] for _ in range(N)]
     for i in range(N):
         for j in deps[i]:

@@ -1,4 +1,3 @@
-from concourse.bass import DstId, RemoteDMATransfer
 from concourse.mybir import AluOpType as OP, AxisListType, ActivationFunctionType as AF
 
 M, L, CAP, VI, ST = 2304, 208, 160, 3, 5
@@ -6,10 +5,10 @@ W = M + (VI - 1) * L
 CW = W + L
 NL, K0 = (112, 96), (0, 112)
 TOP = 16777216
-CYC = 0.00104
-VS = {0: ((0, 28), (28, 56)), 1: ((0, 24), (24, 48))}
-SS = {0: ((56, 84), (84, 112)), 1: ((48, 72), (72, 96))}
-TRIES = [(0.3 * b, 0.3 * (s > 1), 1e-9, s) for b in range(12) for s in range(1, 12)]
+CYC = 0.00095
+VS = {0: ((0, 36), (36, 72)), 1: ((0, 30), (30, 62))}
+SS = {0: ((72, 92), (92, 112)), 1: ((62, 78), (78, 96))}
+TRIES = [(0.2 * b, 0.3 * (s > 1), 1e-9, s) for b in range(20) for s in range(1, 30)]
 
 SCRATCH = {"PT": ("sbuf", [128, W], "bfloat16"), "QA": ("sbuf", [128, VI * L], "bfloat16"), "CH": ("sbuf", [128, CW], "float32"),
            "CHI": ("sbuf", [128, CW], "int32"), "WI": ("sbuf", [128, 1], "int32"), "THI": ("sbuf", [128, 1], "int32"),
@@ -37,16 +36,17 @@ def _pool(dtype, halves, **bufs):
 
 
 _pool("bfloat16", dict(DT=1792, A0=112, ST=16, ST0=112, ST1=112, ST2=112, ST3=112, U=256, UF=256, UG=256, EA=128, EB=128, EC=128,
-                       ED=128), THB=128, ONB=128, IB=128, I25=128, IN=128, R8=8, W8=8, ZC=896, TRI=128, TRP=112, B5=128, MW=24,
-      LG=4 * L, FAR=16, ML=256, ML2=256, MG=L, MGN=L, EE=L, FM=CAP, FQ=CAP, QF1=2 * L, XG0=512, XG1=512, QC1=L, QC2=L)
+                       ED=128, OL=128), THB=128, ONB=128, IB=128, I25=128, IN=128, R8=8, W8=8, ZC=896, TRI=128, TRP=112, MW=24,
+      LG=8 * L, FAR=16, ML=256, ML2=256, ML3=256, MG=L, MGN=L, EE=L, FM=CAP, QF1=L, QF2=L, XG0=512, XG1=512, QC1=L, QC2=L)
 _pool("float32", dict(PF=112, SC1=128, SC2=128, FS=128, FS2=128, NR=8, X=128, Y=128, LB=128, FC=8, FV=8, FX=8, R0S=24, KM0=128,
-                      KM1=128, KM2=128, KM3=128, PA=8, PB=8, PC=8), WF=1, THF=1, ONF=128, IF=128, ICOL=1, C4K=1, LMASK=128,
-      CMASK=8, SEGR=128, KC=16, KC2=16, KJ=16, KN=L, TH=8, LD0=128, LF=128, LS=128, NB=16, S0=16, DA=16, DB=16, DST=16,
-      NOD=16, Z1=16, N1=16, B1=16, GMF=8, BST=16, OUTL=32, GG=L, OB=L, BN=L, CAN=16, DMIN=16, YPL=16, NF=16)
-_pool("int32", dict(SEL=8, ND=8, RBC=8), PI=2, RI=128, BCI=16, H=128, LW=128, LWL=16, SI=32, BEST=16, MI=256, MCI=256, MCJ=256,
-      NCI=16)
+                      KM1=128, KM2=128, KM3=128, PA=8, PB=8, PC=8), WF=1, THF=1, ONF=128, IF=128, ICOL=1, C4K=1, C4K1=1,
+      LMASK=128, CMASK=8, SEGR=128, KC=16, KC2=16, KJ=16, KN=L, TH=8, LD0=128, LF=128, LS=128, NB=16, S0=16, DA=16, DB=16,
+      DST=16, NOD=16, Z1=16, N1=16, B1=16, GMF=8, FARS=16, BST=16, OUTL=32, GG=L, BN=L, BX=L, LOF=16, HIF=16, GD=16, CAN=16,
+      DMIN=16, YPL=16, NF=16)
+_pool("int32", dict(SEL=8, ND=8, RBC=8, ROOT=8, BI=8), PI=2, RI=128, BCI=16, H=128, LW=128, LWL=16, SI=32, BEST=16, MI=256,
+      MCJ=256, NCI=16)
 _pool("uint16", dict(P16=112, LT=8), BCL=8, BCS=8, DL=14, NLT=14, DL2=14)
-SEMAPHORES = ["cv", "cs", "ct", "cg", "arr0", "arr1", "loc0", "loc1"] + ["d%d" % i for i in range(16)]
+SEMAPHORES = ["cv", "cs", "ct", "cg", "aq0", "aq1", "am0", "am1", "lq0", "lq1", "lm0", "lm1"] + ["d%d" % i for i in range(16)]
 PLAN = {}
 
 
@@ -57,8 +57,8 @@ def hop_of(src, dst, cores, topo):
     return ([c for c in fit if topo.die(c) == topo.die(src)] or fit)[0]
 
 
-def some(engines, n):
-    return [sum(1 << e for e in engines[i * n:(i + 1) * n]) for i in range(len(engines) // n)]
+def some(engines):
+    return sum(1 << e for e in engines[:8])
 
 
 def rank_program(g, core, T, topo):
@@ -70,12 +70,12 @@ def rank_program(g, core, T, topo):
             src, dst = cores[r], cores[(r + 1) % n]
             if hop_of(src, dst, cores, topo) == core:
                 rid, pid = topo.addr(dst, core)
-                for t in ("0", "1"):
-                    g.wait_ge(T.sem["arr" + t], 8)
-                    g.remote_dma(T["LAND" + t][:], T["LAND" + t][:], T.sem["arr" + t], T.sem["loc" + t], pid, rid,
-                                 some(topo.engines(core, dst), 8)[0])
-                for t in ("0", "1"):
-                    g.wait_ge(T.sem["loc" + t], 8)
+                for t in ("q0", "m0", "q1", "m1"):
+                    a = T["LAND" + t[1]][:, 0:CAP] if t[0] == "q" else T["LAND" + t[1]][:, CAP:2 * CAP]
+                    g.wait_ge(T.sem["a" + t], 8)
+                    g.remote_dma(a, a, T.sem["a" + t], T.sem["l" + t], pid, rid, some(topo.engines(core, dst)))
+                for t in ("q0", "m0", "q1", "m1"):
+                    g.wait_ge(T.sem["l" + t], 8)
         return
 
     ops, half, ndma, turn = [], [0], [0], [0]
@@ -201,10 +201,13 @@ def rank_program(g, core, T, topo):
     asel(A("IF"), A("ONF"), [[-1, 128]], OP.is_equal, 0.0, 0, 1)
     asel(A("IB"), A("ONB"), [[-1, 128]], OP.is_equal, 0.0, 0, 1)
     Z = lambda b: A("ZC", b * 128, b * 128 + 128)
-    for b in (1, 2, 5, 6):
-        asel(Z(b), Z(b), [[-1, 8], [0, 16]], OP.not_equal, -1.0, -8, 1)
-    for b, c in ((0, 1.0), (1, -1.0), (2, 1.0), (3, -1.0), (4, 1.0)):
-        asel(Z(b), Z(b), [[-1, 8], [0, 16]], OP.not_equal, c, 0, 1)
+    asel(Z(0), Z(0), [[-1, 8], [0, 16]], OP.not_equal, 1.0, 0, 1)
+    asel(Z(5), Z(5), [[-1, 8], [0, 16]], OP.not_equal, -1.0, -8, 1)
+    tt(Z(1), Z(5), Z(0), OP.subtract)
+    tt(Z(2), Z(5), Z(0), OP.add)
+    ts(Z(3), Z(0), -1.0, OP.mult)
+    cp(Z(4), Z(0))
+    cp(Z(6), Z(5))
     for b, sgn, c in ((0, -16, -7.5), (1, 16, 0.0), (2, -16, -15.0)):
         z = A("ZC", b * 128, b * 128 + 128, 1, (32, 34))
         iota(z, [[0, 8], [sgn, 16]], 0, 0, True)
@@ -214,6 +217,7 @@ def rank_program(g, core, T, topo):
     ts(A("PI", 1, 2), A("PI", 0, 1), 15, OP.bitwise_and)
     cp(A("ICOL"), A("PI", 1, 2))
     ts(A("C4K"), A("ICOL"), 4096.0, OP.mult)
+    ts(A("C4K1"), A("C4K"), 1.0, OP.add)
     ts(A("LMASK"), A("RI"), A("ICOL"), OP.is_equal)
     cp(A("BCL"), A("BCI", 0, 8))
     cp(A("BCS"), A("BCI", 8, 16))
@@ -223,6 +227,7 @@ def rank_program(g, core, T, topo):
         for nm in ("SC2", "NR", "Y", "FV", "KM0", "KM1", "KM2"):
             fill(A(nm + h), 0.0)
         fill(A("ND" + h), 0)
+        fill(A("BI" + h), 0)
         for l in "0123":
             fill(A("ST" + l + h), 0.0)
             fill(A("ST" + l + h, 0, 112, 1, (32, 34)), 1.0)
@@ -242,25 +247,24 @@ def rank_program(g, core, T, topo):
     ts(A("IN"), A("IB"), -1.0, OP.mult)
     ts(A("I25"), A("IB"), 33554432.0, OP.mult)
     fill(A("TRP"), 8192.0)
-    for nm in ("B5", "MW"):
+    for nm in ("MW", "ML3"):
         fill(A(nm), 0.0)
-    for nm in ("MI", "MCI", "MCJ"):
+    for nm in ("MI", "MCJ"):
         fill(A(nm), 0)
     cp(A("MI", 4, 256, 16), A("ONF", 0, 16))
-    for nm, j, v in (("MCI", 3, -1.0), ("MCI", 4, -64.0), ("MCJ", 1, 1.0), ("MCJ", 2, 64.0)):
+    for nm, j, v in (("ML3", 3, -1.0), ("ML3", 4, -64.0), ("MCJ", 1, 1.0), ("MCJ", 2, 64.0)):
         ts(A(nm, j, 256, 16), A("ONF", 0, 16), v, OP.mult)
     ts(A("GMF"), A("R8"), 1.0 / 65536, OP.mult)
     for t in (0, 1):
-        fill(A("SEND%d" % t, 208, 368), -1.0)
+        fill(A("SEND%d" % t, 208, 368), -80.0)
         fill(A("SEND%d" % t, 576, 736), 0.0)
-        ts(A("QF1", t * L, t * L + L), A("QA", (t + 1) * L, (t + 2) * L), 1.0, OP.add)
+        ts(A("QF%d" % (t + 1)), A("QA", (t + 1) * L, (t + 2) * L), 64.0, OP.subtract)
         cp(A("QC%d" % (t + 1), CAP, L), A("QA", (t + 1) * L + CAP, (t + 2) * L))
     cp(A("THF"), A("THI"))
     ts(A("THB"), A("ONB"), A("THF"), OP.mult)
     asel(A("TRI"), A("ONB"), [[1, 128]], OP.is_ge, 0.0, -1, -1)
     asel(A("TRI"), A("TRI"), [[1, 128]], OP.not_equal, -512.0, 0, -1)
     asel(A("TRP"), A("TRP"), [[1, 112]], OP.is_ge, 0.0, 0, -1)
-    asel(A("B5"), A("B5"), [[-16, 8], [0, 16]], OP.not_equal, 1.0, -5, 1)
     for c, j, v in ((0, 0, 65536.0), (8, 1, 1.0), (8, 2, 64.0), (8, 3, 4096.0), (16, 4, 1.0)):
         asel(A("MW", c, c + 8), A("MW", c, c + 8), [[-16, 8]], OP.not_equal, v, -j, 1)
     iota(A("KC"), [[112, 2], [0, 8]], 0, 1, True)
@@ -275,6 +279,7 @@ def rank_program(g, core, T, topo):
 
     HB = lambda nm, h, c0=0, c1=None, st=1: A(nm + "_" + str(h), c0, c1, st)
     SI = lambda h, a, b: A("SI", 16 * h + a, 16 * h + b, 1, (0, NL[h]))
+    HI = lambda h, e: A("H", h * 64 + e, h * 64 + 64, 8, (0, NL[h]))
     LAST = lambda nm, h: RW(nm, h, 15, 128, 16)
     SEG = lambda h: A("SEGR", 0, 128, 1, (0, NL[h]))
     EYE = lambda nm, k: A(nm, 0, k, 1, (0, k))
@@ -284,12 +289,12 @@ def rank_program(g, core, T, topo):
         tt(HB("LB", h), ind(win, A("BCL")), A("LMASK"), OP.mult)
         mm(A("KEY%d" % h, 128, 128 + NL[h] // 16), RW("LB", h), A("CMASK", 0, NL[h] // 16, 1, (0, NL[h])))
 
-    def list_copy(out, h):
-        cp(out, A("KEY%d" % h, 128, 128 + NL[h] // 16))
+    def list_copy(out, h, more=0.0):
+        ts(out, A("KEY%d" % h, 128, 128 + NL[h] // 16), more, OP.add)
 
-    def kids(h):
+    def kids(h, more=0.0):
         k = NL[h] // 16
-        list_copy(HB("LT", h, 0, k), h)
+        list_copy(HB("LT", h, 0, k), h, more)
         ts(HB("P16", h, 0, NL[h]), ind(A("CH"), HB("LT", h, 0, k)), A("C4K"), OP.subtract)
         act(HB("PF", h, 0, NL[h]), ind(A("CH"), HB("LT", h, 0, k)), AF.Copy)
 
@@ -349,7 +354,7 @@ def rank_program(g, core, T, topo):
 
     def look(h, s):
         scan(RW("SC1", h), SEG(h), RW("KEY", h, 0, 128), OP.max, OP.min)
-        t1, rho = A("H", h * 64 + s + 1, h * 64 + 64, 8, (0, NL[h])), SI(h, 8, 16)
+        t1, rho = HI(h, s + 1), SI(h, 8, 16)
         tt(t1, LAST("SC1", h), RW("RBC", h) if s == 1 else rho, OP.min)
         if s <= ST:
             ts(RW("NR", h), t1, -float(TOP), OP.mult, -7.5 * 65536 * TOP, OP.add)
@@ -390,20 +395,21 @@ def rank_program(g, core, T, topo):
     for t in range(VI):
         q = lambda a, b: A(QN[t], a, b)
         if t:
-            ld = "LAND%d" % (t - 1)
-            op("x", None, [], [A(ld)], "x", T.sem["arr%d" % (t - 1)], 8)
-            ts(A("FM"), A(ld, 0, CAP), 0.0, OP.is_lt)
-            tt(A("FQ"), A("FM"), A("QF1", (t - 1) * L, (t - 1) * L + CAP), OP.mult)
-            tt(q(0, CAP), A("FQ"), A(ld, 0, CAP), OP.add)
+            ld, fq = "LAND%d" % (t - 1), "QF%d" % t
+            op("x", None, [], [A(ld, 0, CAP)], "x", T.sem["aq%d" % (t - 1)], 8)
+            op("x", None, [], [A(ld, CAP, 2 * CAP)], "x", T.sem["am%d" % (t - 1)], 8)
+            tt(A(fq, 0, CAP), A(fq, 0, CAP), A(ld, 0, CAP), OP.max)
+            ts(A("FM"), A(fq, 0, CAP), 0.0, OP.is_lt, 64.0, OP.mult)
+            tt(q(0, CAP), A("FM"), A(fq, 0, CAP), OP.add)
         for h in (1, 0):
-            mm(RW("KEY", h, 136, 144), q(K0[h], K0[h] + NL[h]), A("W8"))
+            mm(RW("KEY", h, 136, 144), A(fq if t else "QA", K0[h], K0[h] + NL[h]), A("W8"))
             if t:
                 mm(A("KEY%d" % h, 152, 176, 1, (0, nh[h])), A(ld, CAP + K0[h], CAP + K0[h] + nh[h]), A("MW"))
         for h in (1, 0):
             cp(RW("SEL", h), RW("KEY", h, 136, 144))
             ts(RW("ND", h), RW("SEL", h), 63, OP.bitwise_and)
-            ts(RW("ND", h), RW("ND", h), 1, OP.add)
             to_list(HB("ND", h), h)
+            ts(RW("ROOT", h), RW("ND", h), 1, OP.add)
         for i in range(16):
             if i < 10:
                 cp(A("Q16", i, 16 * L, 16), q(0, L))
@@ -425,7 +431,7 @@ def rank_program(g, core, T, topo):
             fill(A("PT", 0, 1), 256.0)
         for h in (1, 0):
             k = NL[h] // 16
-            kids(h)
+            kids(h, 1.0)
             a0 = HB("A0", h, 0, NL[h])
             tt(a0, ind(A("PT"), HB("LT", h, 0, k)), q(K0[h], K0[h] + NL[h]), OP.subtract)
             act(a0, a0, AF.Abs)
@@ -436,7 +442,7 @@ def rank_program(g, core, T, topo):
             masks(h, 0, True, [])
             tt(RW("SEL", h), SI(h, 0, 8), SI(h, 8, 16), OP.is_lt)
             tt(RW("RBC", h), SI(h, 0, 8), SI(h, 8, 16), OP.min)
-            tt(A("H", h * 64 + 1, h * 64 + 64, 8, (0, NL[h])), RW("SEL", h), RW("ND", h), OP.mult)
+            tt(HI(h, 1), RW("SEL", h), RW("ROOT", h), OP.mult)
         for h in (1, 0):
             points(h)
             keys(h)
@@ -457,7 +463,7 @@ def rank_program(g, core, T, topo):
         both = lambda nm: A(nm, 0, 16)
         if not last:
             for h in (1, 0):
-                tt(hc("FAR", h), SI(h, 8, 16), A("TH", 0, 8, 1, (0, NL[h])), OP.is_ge)
+                tt(hc("FAR", h), HI(h, 7), A("TH", 0, 8, 1, (0, NL[h])), OP.is_ge)
             mm(RW("FB", 0, 0, 8), EYE("TRI", 112), hc("FAR", 0))
             mm(RW("FB", 1, 0, 8), EYE("TRI", 96), hc("FAR", 1), True, False)
             mm(RW("FB", 1, 0, 8), A("ONB", 0, 96, 1, (0, 112)), hc("FAR", 0), False, True)
@@ -493,8 +499,7 @@ def rank_program(g, core, T, topo):
             w1, w2 = (ind(A("SEND%d" % t, a, a + 368), A("DL", 0, 13)) for a in (0, 368))
             cp(w1, q(0, L))
             for h in (1, 0):
-                for j, k in ((0, 16), (5, 20)):
-                    ts(A("MI", 128 * h + j, 128 * h + 128, 16, (0, NL[h])), SI(h, 8, 16), k, OP.logical_shift_right)
+                ts(A("MI", 128 * h, 128 * h + 128, 16, (0, NL[h])), SI(h, 8, 16), 16, OP.logical_shift_right)
             cp(both("BEST"), both("BST"))
             ts(A("MI", 1, 256, 16), both("BEST"), 63, OP.bitwise_and)
             ts(A("MI", 2, 256, 16), both("BEST"), 6, OP.logical_shift_right, 63, OP.bitwise_and)
@@ -510,12 +515,14 @@ def rank_program(g, core, T, topo):
             dst = cores[(rank + 1) % n]
             hop = hop_of(core, dst, cores, topo)
             rid, pid = topo.addr(hop, core)
-            m = some(topo.engines(core, hop), 4)
-            tr = [RemoteDMATransfer(dst_ids=[DstId(rid=rid, pnc=pid)], dma_engine_mask=m[i], remote_sem=T.sem["arr%d" % t],
-                                    src=T["SEND%d" % t][:, a:a + CAP], dst=T["LAND%d" % t][:, i * CAP:(i + 1) * CAP])
-                  for i, a in ((0, 208), (1, 576))]
-            op("g", lambda tr=tr, t=t: g.remote_dma_fused(tr, local_sem=T.sem["loc%d" % t]), [A("SEND%d" % t)], [], "r",
-               T.sem["loc%d" % t], 8, 1.0)
+            m = some(topo.engines(core, hop))
+
+            def send(x, a, b):
+                s, d = A("SEND%d" % t, a, a + CAP), A("LAND%d" % t, b, b + CAP)
+                ra, rl = T.sem["a%s%d" % (x, t)], T.sem["l%s%d" % (x, t)]
+                op("g", lambda: g.remote_dma(d[0], s[0], ra, rl, pid, rid, m), [s], [], "r", rl, 8, 1.0)
+            send("q", 208, 0)
+            send("m", 576, CAP)
         for h in (1, 0):
             ts(A("OUTL", 16 * h, 16 * h + 8, 1, (0, NL[h])), SI(h, 8, 16), 1.0 / 65536, OP.mult)
             cp(A("OUTL", 16 * h + 8, 16 * h + 16, 1, (0, NL[h])), hc("BST", h))
@@ -532,30 +539,41 @@ def rank_program(g, core, T, topo):
         for h in (1, 0):
             list_copy(A("NLT", 7 * h, 7 * h + NL[h] // 16), h)
         act(A("GG"), ind(A("CH"), A("NLT", 0, 13)), AF.Copy)
-        mm(A("ZB0", 256, 256 + L), A("B5"), A("MG"))
-        ts(A("OB"), A("ZB0", 256, 256 + L), A("ICOL"), OP.is_equal)
+        for h in (1, 0):
+            ts(RW("BI", h), HI(h, 7), 20, OP.logical_shift_right)
+            tt(HB("OL", h), ind(HB("BI", h), A("BCL")), A("RI"), OP.is_equal)
+            mm(A("ZB0", 256 + K0[h], 256 + K0[h] + NL[h]), RW("OL", h), EYE("IB", NL[h]))
+        ob = A("ZB0", 256, 256 + L)
         ts(A("BN"), A("KN"), float(t * L), OP.add)
-        tt(A("BN"), A("BN"), A("OB"), OP.mult)
-        ts(A("EE"), A("GG"), A("C4K"), OP.is_equal)
-        tt(A("EE"), A("EE"), A("OB"), OP.mult)
+        tt(A("BN"), A("BN"), ob, OP.mult)
+        ts(A("BX"), ob, A("C4K1"), OP.mult, -1.0, OP.add)
+        tt(A("EE"), A("GG"), A("BX"), OP.is_equal)
         for h in (1, 0):
             mm(RW("SP", h, 0, 8), A("EE", K0[h], K0[h] + NL[h]), A("R8"))
-        tt(both("YPL"), both("FAR"), both("NOD"), OP.mult)
-        for h in (1, 0):
-            ts(hc("CAN", h), RW("SP", h, 0, 8), 1.0 / 65536, OP.mult)
-        tt(both("YPL"), both("YPL"), both("CAN"), OP.mult)
-        cp(both("NCI"), both("YPL"))
-        for nm, ml, j in (("MCI", "ML", 1), ("MCJ", "ML2", 3)):
-            ts(A(nm, j, 256, 16), both("NCI"), 63, OP.bitwise_and)
-            ts(A(nm, j + 1, 256, 16), both("NCI"), 6, OP.logical_shift_right)
-            cp(A(ml), A(nm))
-        to_gp()
+        cp(both("NCI"), both("NOD"))
+        ts(A("MCJ", 3, 256, 16), both("NCI"), 63, OP.bitwise_and)
+        ts(A("MCJ", 4, 256, 16), both("NCI"), 6, OP.logical_shift_right)
+        cp(A("ML2"), A("MCJ"))
         to_gp("ZB1", "ML2")
-        act(A("MG"), A("ZB0", 0, L), AF.Copy)
         act(A("MGN"), A("ZB1", 0, L), AF.Copy)
+        ts(both("FARS"), both("FAR"), 1.0 / 65536, OP.mult)
+        tt(both("LOF"), A("MCJ", 3, 256, 16), both("FARS"), OP.mult)
+        tt(both("HIF"), A("MCJ", 4, 256, 16), both("FARS"), OP.mult)
+        tt(both("YPL"), both("FARS"), both("NOD"), OP.mult)
+        for h in (1, 0):
+            for j, nm in ((1, "LOF"), (2, "HIF")):
+                tt(A("ML3", 128 * h + j, 128 * h + 128, 16, (0, NL[h])), RW("SP", h, 0, 8), hc(nm, h), OP.mult)
+        to_gp("ZB0", "ML3")
+        act(A("MG"), A("ZB0", 0, L), AF.Copy)
+        for h in (1, 0):
+            cp(hc("CAN", h), RW("SP", h, 0, 8))
+        tt(both("YPL"), both("YPL"), both("CAN"), OP.mult)
+        ts(both("DA"), both("YPL"), 0.0, OP.is_gt)
+        tt(both("DA"), both("DA"), both("KJ"), OP.mult)
+        tt(both("GD"), both("YPL"), both("DA"), OP.subtract)
         banks, z = ("FB0", "FB1", "ZB0", "ZB1"), 0
         for gr in range(8):
-            lg = gr % 4 * L
+            lg = gr * L
             ts(A("LG", lg, lg + L), A("MGN"), A("GMF", gr, gr + 1), OP.mult)
             for h in (1, 0):
                 nl, w = NL[h], K0[h] + NL[h]
@@ -565,10 +583,9 @@ def rank_program(g, core, T, topo):
                 mm(A(o[1], K0[h], w, 1, (0, nl)), EYE("IB", nl), A("TRP", 0, nl, 1, (0, nl)), False, True)
                 least(A("DMIN", 8 * h + gr, 8 * h + gr + 1, 1, (0, nl)), o)
         ts(both("DMIN"), both("DMIN"), 0.0, OP.is_gt)
+        tt(both("GD"), both("GD"), both("DMIN"), OP.mult)
+        tt(both("DST"), both("KJ"), both("GD"), OP.add)
         tt(both("YPL"), both("YPL"), both("DMIN"), OP.mult)
-        ts(both("DA"), both("YPL"), 0.0, OP.is_equal)
-        tt(both("DA"), both("DA"), both("KJ"), OP.mult)
-        tt(both("DST"), both("DA"), both("YPL"), OP.add)
         for h in (1, 0):
             to_list(A("DST", 8 * h, 8 * h + 8), h)
         for h in (1, 0):
@@ -606,7 +623,7 @@ def plan(ops):
             dep.update(pool[-1:])
             pool.append(i)
         if kind == "x":
-            dep.add(sent[-1])
+            dep.add(sent[-2 if ops[i - 1][4] != "x" else -1])
         if kind == "r":
             sent.append(i)
         deps.append(dep)
@@ -618,7 +635,7 @@ def plan(ops):
                 elif w and r[6] == 1:
                     h[:] = [e for e in h if not (r[2] <= e[1][2] and e[1][3] <= r[3] and r[4] <= e[1][4] and e[1][5] <= r[5])]
                 h.append((i, r, w))
-    after = [{"c": 0.12, "d": 2.2, "r": 7.5, "x": 0.1}[o[4]] for o in ops]
+    after = [{"c": 0.18, "d": 2.2, "r": 6.0, "x": 0.1}[o[4]] for o in ops]
     nxt = [[] for _ in range(N)]
     for i in range(N):
         for j in deps[i]:

from concourse.mybir import AluOpType as OP, AxisListType, ActivationFunctionType as AF

M, L, CAP, VI, ST = 2304, 208, 160, 3, 5
W = M + (VI - 1) * L
CW = W + L
NL, K0 = (112, 96), (0, 112)
TOP = 16777216
CYC = 0.00095
VS = {0: ((0, 36), (36, 72)), 1: ((0, 30), (30, 62))}
SS = {0: ((72, 92), (92, 112)), 1: ((62, 78), (78, 96))}
TRIES = [(0.2 * b, 0.3 * (s > 1), 1e-9, s) for b in range(20) for s in range(1, 30)]

SCRATCH = {"PT": ("sbuf", [128, W], "bfloat16"), "QA": ("sbuf", [128, VI * L], "bfloat16"), "CH": ("sbuf", [128, CW], "float32"),
           "CHI": ("sbuf", [128, CW], "int32"), "WI": ("sbuf", [128, 1], "int32"), "THI": ("sbuf", [128, 1], "int32"),
           "Q16": ("sbuf", [128, 16 * L], "bfloat16"), "R0I": ("sbuf", [8, VI * L], "int32"),
           "R0F": ("sbuf", [8, VI * L], "float32"), "YO": ("sbuf", [16, VI * L], "float32"), "YPO": ("sbuf", [8, 2 * L], "float32")}
for _h in ("0", "1"):
    SCRATCH["SEND" + _h] = ("sbuf", [128, 736], "bfloat16")
    SCRATCH["LAND" + _h] = ("sbuf", [128, 2 * CAP], "bfloat16")
    for _n in ("KEY", "ZB", "FB", "SP"):
        SCRATCH[_n + _h] = ("psum", [128, 512], "float32")
PSUMS = {n for n in SCRATCH if SCRATCH[n][0] == "psum"}
SIZES = {n: (SCRATCH[n][1], SCRATCH[n][2]) for n in SCRATCH}
POOL = {}


def _pool(dtype, halves, **bufs):
    big, at = "ALL" + dtype[0], 0
    for two, group in ((False, bufs), (True, halves)):
        for k in group:
            for name in ([k + "_0", k + "_1"] if two else [k]):
                POOL[name] = (big, at)
                SIZES[name] = ([128, group[k]], dtype)
                at += (group[k] + 15) // 16 * 16
    SCRATCH[big] = ("sbuf", [128, at], dtype)


_pool("bfloat16", dict(DT=1792, A0=112, ST=16, ST0=112, ST1=112, ST2=112, ST3=112, U=256, UF=256, UG=256, EA=128, EB=128, EC=128,
                       ED=128, OL=128), THB=128, ONB=128, IB=128, I25=128, IN=128, R8=8, W8=8, ZC=896, TRI=128, TRP=112, MW=24,
      LG=8 * L, FAR=16, ML=256, ML2=256, ML3=256, MG=L, MGN=L, EE=L, FM=CAP, QF1=L, QF2=L, XG0=512, XG1=512, QC1=L, QC2=L)
_pool("float32", dict(PF=112, SC1=128, SC2=128, FS=128, FS2=128, NR=8, X=128, Y=128, LB=128, FC=8, FV=8, FX=8, R0S=24, KM0=128,
                      KM1=128, KM2=128, KM3=128, PA=8, PB=8, PC=8), WF=1, THF=1, ONF=128, IF=128, ICOL=1, C4K=1, C4K1=1,
      LMASK=128, CMASK=8, SEGR=128, KC=16, KC2=16, KJ=16, KN=L, TH=8, LD0=128, LF=128, LS=128, NB=16, S0=16, DA=16, DB=16,
      DST=16, NOD=16, Z1=16, N1=16, B1=16, GMF=8, FARS=16, BST=16, OUTL=32, GG=L, BN=L, BX=L, LOF=16, HIF=16, GD=16, CAN=16,
      DMIN=16, YPL=16, NF=16)
_pool("int32", dict(SEL=8, ND=8, RBC=8, ROOT=8, BI=8), PI=2, RI=128, BCI=16, H=128, LW=128, LWL=16, SI=32, BEST=16, MI=256,
      MCJ=256, NCI=16)
_pool("uint16", dict(P16=112, LT=8), BCL=8, BCS=8, DL=14, NLT=14, DL2=14)
SEMAPHORES = ["cv", "cs", "ct", "cg", "aq0", "aq1", "am0", "am1", "lq0", "lq1", "lm0", "lm1"] + ["d%d" % i for i in range(16)]
PLAN = {}


def hop_of(src, dst, cores, topo):
    if topo.may_write(src, dst):
        return dst
    fit = [c for c in topo.cores_of(src) if c not in cores and topo.may_write(c, dst)]
    return ([c for c in fit if topo.die(c) == topo.die(src)] or fit)[0]


def some(engines):
    return sum(1 << e for e in engines[:8])


def rank_program(g, core, T, topo):
    rank = T.rank_of(core)
    cores = list(T.cores)
    n = len(cores)
    if rank is None:
        for r in range(n):
            src, dst = cores[r], cores[(r + 1) % n]
            if hop_of(src, dst, cores, topo) == core:
                rid, pid = topo.addr(dst, core)
                for t in ("q0", "m0", "q1", "m1"):
                    a = T["LAND" + t[1]][:, 0:CAP] if t[0] == "q" else T["LAND" + t[1]][:, CAP:2 * CAP]
                    g.wait_ge(T.sem["a" + t], 8)
                    g.remote_dma(a, a, T.sem["a" + t], T.sem["l" + t], pid, rid, some(topo.engines(core, dst)))
                for t in ("q0", "m0", "q1", "m1"):
                    g.wait_ge(T.sem["l" + t], 8)
        return

    ops, half, ndma, turn = [], [0], [0], [0]
    QUE = {"v": g.vector, "s": g.scalar, "t": g.tensor, "g": g, "y": g.sync}
    SEM = {"v": T.sem.cv, "s": T.sem.cs, "t": T.sem.ct, "g": T.sem.cg}

    def A(name, c0=0, c1=None, st=1, p=(0, None)):
        shp, (b, o) = SIZES[name][0], POOL.get(name, (name, 0))
        c1 = shp[1] if c1 is None else c1
        p1 = shp[0] if p[1] is None else p[1]
        x = T[b][p[0]:p1, o + c0:o + c1:st] if st > 1 else T[b][p[0]:p1, o + c0:o + c1]
        return (x, name, p[0], p1, c0, c1, st)

    def ind(win, off):
        return ("I", win, off)

    def is_ind(x):
        return isinstance(x[0], str)

    def ap(x):
        return x[1][0].indirect(x[2][0]) if is_ind(x) else x[0]

    def size(x):
        return 16 * (x[2][5] - x[2][4]) if is_ind(x) else (x[5] - x[4] + x[6] - 1) // x[6]

    def cost(q, what, out, ins):
        m = size(out)
        if q == "v":
            if is_ind(out):
                return 0.05 + m * 3.5 * CYC
            if any(is_ind(x) for x in ins):
                return 0.05 + m * 1.5 * CYC
            if what == "tt":
                m *= 1 if any(x[1] in PSUMS for x in ins) else 2
            elif what == "red":
                m = size(ins[0])
            elif what != "scan" and all(SIZES[x[1]][1] in ("bfloat16", "uint16") for x in [out] + list(ins)):
                m *= 0.5
            return max(64, m) * CYC
        if q == "s":
            return 0.065 + m * (1.5 if is_ind(ins[0]) else 1) * CYC
        if q == "t":
            return max(min(64, size(ins[0])), m) * 0.0007 * (4 if SIZES[ins[0][1]][1] == "float32" else 1)
        return 0.15 + 2 * m * CYC

    def op(q, fn, rd, wr, kind="c", sem=None, val=1, c=0.1):
        R, Wr = [], []
        for x in rd:
            R += [x[1], x[2]] if is_ind(x) else [x]
        for x in wr:
            Wr.append(x[1] if is_ind(x) else x)
            if is_ind(x):
                R.append(x[2])
        ops.append((q, fn, R, Wr, kind, sem, val, c, half[0]))

    def call(q, what, fn, out, *ins):
        op(q, fn, ins, [out], c=cost(q, what, out, ins))

    def dma(q, out, in_, rd, wr):
        s = T.sem["d%d" % ndma[0]]
        ndma[0] += 1
        op(q, lambda: QUE[q].dma_start(out, in_), rd, wr, "d", s, 16)

    def load(q, name, src, a=0, b=None):
        dma(q, A(name, a, b)[0], src, [], [A(name, a, b)])

    def tt(out, a, b, o):
        call("v", "tt", lambda: g.vector.tensor_tensor(ap(out), ap(a), ap(b), o), out, a, b)

    def ts(out, a, s1, o0, s2=None, o1=None):
        rd = [a] + [x for x in (s1, s2) if isinstance(x, tuple)]
        v1, v2 = (ap(x) if isinstance(x, tuple) else x for x in (s1, s2))
        more = () if o1 is None else (o1,)
        op("v", lambda: g.vector.tensor_scalar(ap(out), ap(a), v1, v2, o0, *more), rd, [out], c=cost("v", "ts", out, [a]))

    def cp(out, a):
        call("v", "cp", lambda: g.vector.tensor_copy(ap(out), ap(a)), out, a)

    def fill(out, c):
        call("v", "fill", lambda: g.vector.memset(ap(out), c), out)

    def scan(out, d0, d1, o0, o1):
        call("v", "scan", lambda: g.vector.tensor_tensor_scan(ap(out), ap(d0), ap(d1), 0.0, o0, o1), out, d0, d1)

    def least(out, a):
        call("v", "red", lambda: g.vector.tensor_reduce(ap(out), ap(a), AxisListType.X, OP.min, apply_absolute_value=True), out, a)

    def act(out, a, f, scale=1.0):
        call("s", "", lambda: g.scalar.activation(ap(out), ap(a), f, scale=scale), out, a)

    def mm(out, l, r, start=True, stop=True):
        call("t", "", lambda: g.tensor.matmul(ap(out), ap(l), ap(r), start, stop), out, l, r)

    def iota(out, pat, base, cm, small=False):
        kw = {"allow_small_or_imprecise_dtypes": True} if small else {}
        call("g", "", lambda: g.iota(ap(out), pat, base, cm, **kw), out)

    def asel(out, a, pat, cmp, fillv, base, cm):
        call("g", "", lambda: g.affine_select(ap(out), ap(a), pat, cmp, fillv, base, cm), out, a)

    load("y", "WI", T.w[:])
    load("y", "QA", T.q[:, 0:L], 0, L)
    load("s", "R0I", T.r0[:])
    load("s", "CHI", T.ch[:, 0:1152], 0, 1152)
    load("y", "PT", T.pt[:], 0, M)
    load("s", "CHI", T.ch[:, 1152:M], 1152, M)
    load("y", "THI", T.th[:])
    load("y", "QA", T.q[:, L:VI * L], L, VI * L)

    fill(A("R8"), 65536.0)
    fill(A("ONF"), 1.0)
    fill(A("ONB"), 1.0)
    fill(A("SEGR"), 0.0)
    fill(A("ZC"), 0.0)
    iota(A("PI", 0, 1), [[0, 1]], 0, 1)
    iota(A("RI"), [[0, 8], [1, 16]], 0, 0)
    asel(A("R8"), A("R8"), [[-16, 8]], OP.is_ge, 0.0, 0, 1)
    asel(A("R8"), A("R8"), [[16, 8]], OP.is_ge, 0.0, 15, -1)
    asel(A("CMASK"), A("ONF", 0, 8), [[-16, 8]], OP.is_ge, 0.0, 0, 1)
    asel(A("CMASK"), A("CMASK"), [[16, 8]], OP.is_ge, 0.0, 15, -1)
    iota(A("BCI", 0, 8), [[1, 8]], 0, 0)
    iota(A("BCI", 8, 16), [[16, 8]], 15, 0)
    asel(A("IF"), A("ONF"), [[-1, 128]], OP.is_equal, 0.0, 0, 1)
    asel(A("IB"), A("ONB"), [[-1, 128]], OP.is_equal, 0.0, 0, 1)
    Z = lambda b: A("ZC", b * 128, b * 128 + 128)
    asel(Z(0), Z(0), [[-1, 8], [0, 16]], OP.not_equal, 1.0, 0, 1)
    asel(Z(5), Z(5), [[-1, 8], [0, 16]], OP.not_equal, -1.0, -8, 1)
    tt(Z(1), Z(5), Z(0), OP.subtract)
    tt(Z(2), Z(5), Z(0), OP.add)
    ts(Z(3), Z(0), -1.0, OP.mult)
    cp(Z(4), Z(0))
    cp(Z(6), Z(5))
    for b, sgn, c in ((0, -16, -7.5), (1, 16, 0.0), (2, -16, -15.0)):
        z = A("ZC", b * 128, b * 128 + 128, 1, (32, 34))
        iota(z, [[0, 8], [sgn, 16]], 0, 0, True)
        asel(z, z, [[0, 128]], OP.not_equal, c, -1, 1)
    cp(A("ZC", 640, 896, 1, (32, 34)), A("ZC", 128, 384, 1, (32, 34)))
    asel(A("SEGR"), A("SEGR"), [[0, 8], [1, 16]], OP.not_equal, float(TOP), 0, 0)
    ts(A("PI", 1, 2), A("PI", 0, 1), 15, OP.bitwise_and)
    cp(A("ICOL"), A("PI", 1, 2))
    ts(A("C4K"), A("ICOL"), 4096.0, OP.mult)
    ts(A("C4K1"), A("C4K"), 1.0, OP.add)
    ts(A("LMASK"), A("RI"), A("ICOL"), OP.is_equal)
    cp(A("BCL"), A("BCI", 0, 8))
    cp(A("BCS"), A("BCI", 8, 16))
    cp(A("WF"), A("WI"))
    ts(A("W8"), A("R8"), 1.0 / 65536, OP.mult, A("WF"), OP.mult)
    for h in ("_1", "_0"):
        for nm in ("SC2", "NR", "Y", "FV", "KM0", "KM1", "KM2"):
            fill(A(nm + h), 0.0)
        fill(A("ND" + h), 0)
        fill(A("BI" + h), 0)
        for l in "0123":
            fill(A("ST" + l + h), 0.0)
            fill(A("ST" + l + h, 0, 112, 1, (32, 34)), 1.0)
    fill(A("SI"), 0)
    fill(A("H"), 0)
    cp(A("H", 0, 128, 8), A("ONF", 0, 16))
    for nm in ("NB", "DST", "S0", "DB", "FAR", "CAN", "DMIN"):
        fill(A(nm), 0.0)
    fill(A("PT", M, W), 0.0)
    fill(A("CHI", M, CW), 0)
    cp(A("R0F"), A("R0I"))
    for h in (1, 0):
        for t in range(VI):
            a = t * L + K0[h]
            mm(A("FB%d" % h, 8 * t, 8 * t + 8, 1, (0, NL[h])), A("R0F", a, a + NL[h]), A("IF", 0, 8, 1, (0, 8)))
        ts(A("R0S_%d" % h, 0, 24, 1, (0, NL[h])), A("FB%d" % h, 0, 24, 1, (0, NL[h])), 65536.0, OP.mult)
    ts(A("IN"), A("IB"), -1.0, OP.mult)
    ts(A("I25"), A("IB"), 33554432.0, OP.mult)
    fill(A("TRP"), 8192.0)
    for nm in ("MW", "ML3"):
        fill(A(nm), 0.0)
    for nm in ("MI", "MCJ"):
        fill(A(nm), 0)
    cp(A("MI", 4, 256, 16), A("ONF", 0, 16))
    for nm, j, v in (("ML3", 3, -1.0), ("ML3", 4, -64.0), ("MCJ", 1, 1.0), ("MCJ", 2, 64.0)):
        ts(A(nm, j, 256, 16), A("ONF", 0, 16), v, OP.mult)
    ts(A("GMF"), A("R8"), 1.0 / 65536, OP.mult)
    for t in (0, 1):
        fill(A("SEND%d" % t, 208, 368), -80.0)
        fill(A("SEND%d" % t, 576, 736), 0.0)
        ts(A("QF%d" % (t + 1)), A("QA", (t + 1) * L, (t + 2) * L), 64.0, OP.subtract)
        cp(A("QC%d" % (t + 1), CAP, L), A("QA", (t + 1) * L + CAP, (t + 2) * L))
    cp(A("THF"), A("THI"))
    ts(A("THB"), A("ONB"), A("THF"), OP.mult)
    asel(A("TRI"), A("ONB"), [[1, 128]], OP.is_ge, 0.0, -1, -1)
    asel(A("TRI"), A("TRI"), [[1, 128]], OP.not_equal, -512.0, 0, -1)
    asel(A("TRP"), A("TRP"), [[1, 112]], OP.is_ge, 0.0, 0, -1)
    for c, j, v in ((0, 0, 65536.0), (8, 1, 1.0), (8, 2, 64.0), (8, 3, 4096.0), (16, 4, 1.0)):
        asel(A("MW", c, c + 8), A("MW", c, c + 8), [[-16, 8]], OP.not_equal, v, -j, 1)
    iota(A("KC"), [[112, 2], [0, 8]], 0, 1, True)
    iota(A("KC2"), [[-112, 2], [0, 8]], 720, -1, True)
    iota(A("KJ"), [[112, 2], [0, 8]], W, 1, True)
    iota(A("KN"), [[1, L]], M, 0, True)
    mm(A("FB1", 64, 72), A("THB"), A("R8"))
    ts(A("TH"), A("FB1", 64, 72), 1.0 / 16, OP.mult)

    def RW(nm, h, c0=0, c1=None, st=1):
        return A(nm + str(h) if nm + str(h) in PSUMS else nm + "_" + str(h), c0, c1, st, (0, NL[h]))

    HB = lambda nm, h, c0=0, c1=None, st=1: A(nm + "_" + str(h), c0, c1, st)
    SI = lambda h, a, b: A("SI", 16 * h + a, 16 * h + b, 1, (0, NL[h]))
    HI = lambda h, e: A("H", h * 64 + e, h * 64 + 64, 8, (0, NL[h]))
    LAST = lambda nm, h: RW(nm, h, 15, 128, 16)
    SEG = lambda h: A("SEGR", 0, 128, 1, (0, NL[h]))
    EYE = lambda nm, k: A(nm, 0, k, 1, (0, k))
    hc = lambda nm, h, r=None: A(nm, 8 * h, 8 * h + 8, 1, (0, NL[h] if r is None else r))

    def to_list(win, h):
        tt(HB("LB", h), ind(win, A("BCL")), A("LMASK"), OP.mult)
        mm(A("KEY%d" % h, 128, 128 + NL[h] // 16), RW("LB", h), A("CMASK", 0, NL[h] // 16, 1, (0, NL[h])))

    def list_copy(out, h, more=0.0):
        ts(out, A("KEY%d" % h, 128, 128 + NL[h] // 16), more, OP.add)

    def kids(h, more=0.0):
        k = NL[h] // 16
        list_copy(HB("LT", h, 0, k), h, more)
        ts(HB("P16", h, 0, NL[h]), ind(A("CH"), HB("LT", h, 0, k)), A("C4K"), OP.subtract)
        act(HB("PF", h, 0, NL[h]), ind(A("CH"), HB("LT", h, 0, k)), AF.Copy)

    def masks(h, lev, want_y, fbs):
        nl = NL[h]
        stt = lambda l, k=34: A("ST%d_%d" % (min(l, 3), h), 0, nl, 1, (0, k))
        mm(A("ZB%d" % h, 384, 384 + nl, 1, (0, 16)), RW("ST", h), EYE("IB", nl))
        act(stt(lev, 16), A("ZB%d" % h, 384, 384 + nl, 1, (0, 16)), AF.Copy)
        mm(RW("ZB", h, 0, 384), stt(lev), A("ZC", 0, 384, 1, (0, 34)))
        act(RW("U", h), RW("ZB", h, 128, 384), AF.Relu, float(TOP))
        if want_y:
            act(RW("Y", h), RW("ZB", h, 0, 128), AF.Abs, 65536.0 * TOP)
        for c, u, l, k, es in fbs:
            mm(RW("FB", h, 128, 384), stt(l), A("ZC", 384, 640, 1, (0, 34)), True, False)
            mm(RW("FB", h, 128, 384), stt(lev), A("ZC", 640, 896, 1, (0, 34)), False, True)
            act(RW(u, h), RW("FB", h, 128, 384), AF.Relu, float(TOP))

    def fallback(h, fbs):
        for c, u, l, k, es in fbs:
            o = RW("FB", h, c, c + 128)
            mm(o, EYE("IF", NL[h]), RW(k, h), True, False)
            for e in es:
                mm(o, EYE("I25", NL[h]), RW(e, h), False, False)
            mm(o, EYE("IB", NL[h]), RW(u, h, 0, 128), False, False)
            mm(o, EYE("IB", NL[h]), RW(u, h, 128, 256), False, True)

    def points_scalar(h, a, b):
        z = turn[0] = 1 - turn[0]
        w = 16 * (b - a)
        x, o = A("XG%d" % z, 0, w), A("SP%d" % z, 0, w)
        act(x, ind(A("PT"), HB("P16", h, a, b)), AF.Copy)
        mm(o, A("IN"), A("Q16", 16 * (K0[h] + a), 16 * (K0[h] + b)), True, False)
        mm(o, A("IB"), x, False, True)
        act(HB("DT", h, 16 * a, 16 * b), o, AF.Abs)

    def points_vector(h, a, b):
        d = HB("DT", h, 16 * a, 16 * b)
        tt(d, ind(A("PT"), HB("P16", h, a, b)), A("Q16", 16 * (K0[h] + a), 16 * (K0[h] + b)), OP.subtract)
        act(d, d, AF.Abs)

    def points(h):
        for (a, b), (c, d) in zip(VS[h], SS[h]):
            points_scalar(h, c, d)
            points_vector(h, a, b)

    def keys(h):
        nl = NL[h]
        o = RW("KEY", h, 0, 128)
        mm(o, HB("PF", h, 0, nl), A("IF"), True, False)
        mm(o, EYE("IB", nl), RW("U", h, 0, 128), False, False)
        mm(o, EYE("IB", nl), RW("U", h, 128, 256), False, False)
        for i in range(16):
            mm(RW("KEY", h, i, 128, 16), HB("DT", h, i, 16 * nl, 16), A("R8"), False, i == 15)

    FBS = {2: [(0, "UF", 0, "KM0", ("EA",))], 3: [(0, "UF", 1, "KM1", ("EB",))],
           4: [(0, "UF", 2, "KM2", ("EC",)), (384, "UG", 0, "KM0", ("EA", "ED"))]}

    def look(h, s):
        scan(RW("SC1", h), SEG(h), RW("KEY", h, 0, 128), OP.max, OP.min)
        t1, rho = HI(h, s + 1), SI(h, 8, 16)
        tt(t1, LAST("SC1", h), RW("RBC", h) if s == 1 else rho, OP.min)
        if s <= ST:
            ts(RW("NR", h), t1, -float(TOP), OP.mult, -7.5 * 65536 * TOP, OP.add)
        ts(rho, t1, 16711680, OP.bitwise_and)
        if s == ST + 1:
            return
        tt(HB("X", h), ind(HB("NR", h), A("BCL")), HB("Y", h), OP.add)
        km = "KM%d" % min(s - 1, 3)
        tt(RW(km, h), RW("KEY", h, 0, 128), RW("X", h), OP.max)
        scan(RW("SC2", h), SEG(h), RW(km, h), OP.max, OP.min)
        if s >= 3:
            scan(RW("FS", h), SEG(h), RW("FB", h, 0, 128), OP.max, OP.min)
            fc = LAST("FS", h)
            if s == 5:
                scan(RW("FS2", h), SEG(h), RW("FB", h, 384, 512), OP.max, OP.min)
                tt(RW("FX", h), RW("PA", h), RW("PB", h), OP.min)
                tt(RW("FX", h), RW("FX", h), LAST("FS2", h), OP.max)
                tt(RW("FC", h), RW("FX", h), fc, OP.min)
                fc = RW("FC", h)
            tt(RW("FV", h), fc, RW({3: "PA", 4: "PB", 5: "PC"}[s], h), OP.max)
            tt(RW("SEL", h), LAST("SC2", h), RW("FV", h), OP.min)
        else:
            cp(RW("SEL", h), LAST("SC2", h))
        ts(RW("ND", h), RW("SEL", h), 4095, OP.bitwise_and)
        to_list(HB("ND", h), h)
        ts(SI(h, 0, 8), RW("SEL", h), 33488896, OP.bitwise_and)
        ts(RW("ST", h), SI(h, 0, 16), 1.0 / 65536, OP.mult)
        masks(h, s, s < ST, FBS.get(s, []))
        if s in (2, 3, 4):
            ts(RW({2: "PA", 3: "PB", 4: "PC"}[s], h), RW("SEL", h), TOP, OP.is_lt, float(TOP), OP.mult)
        if s <= 3:
            tt(HB({1: "EA", 2: "EB", 3: "EC"}[s], h), ind(HB("SC2", h), A("BCS")), HB(km, h), OP.is_equal)
        if s == 3:
            tt(HB("ED", h), ind(HB("FV", h), A("BCL")), HB("KM0", h), OP.is_equal)

    QN = ("QA", "QC1", "QC2")
    nh = (112, CAP - 112)
    for t in range(VI):
        q = lambda a, b: A(QN[t], a, b)
        if t:
            ld, fq = "LAND%d" % (t - 1), "QF%d" % t
            op("x", None, [], [A(ld, 0, CAP)], "x", T.sem["aq%d" % (t - 1)], 8)
            op("x", None, [], [A(ld, CAP, 2 * CAP)], "x", T.sem["am%d" % (t - 1)], 8)
            tt(A(fq, 0, CAP), A(fq, 0, CAP), A(ld, 0, CAP), OP.max)
            ts(A("FM"), A(fq, 0, CAP), 0.0, OP.is_lt, 64.0, OP.mult)
            tt(q(0, CAP), A("FM"), A(fq, 0, CAP), OP.add)
        for h in (1, 0):
            mm(RW("KEY", h, 136, 144), A(fq if t else "QA", K0[h], K0[h] + NL[h]), A("W8"))
            if t:
                mm(A("KEY%d" % h, 152, 176, 1, (0, nh[h])), A(ld, CAP + K0[h], CAP + K0[h] + nh[h]), A("MW"))
        for h in (1, 0):
            cp(RW("SEL", h), RW("KEY", h, 136, 144))
            ts(RW("ND", h), RW("SEL", h), 63, OP.bitwise_and)
            to_list(HB("ND", h), h)
            ts(RW("ROOT", h), RW("ND", h), 1, OP.add)
        for i in range(16):
            if i < 10:
                cp(A("Q16", i, 16 * L, 16), q(0, L))
            else:
                act(A("Q16", i, 16 * L, 16), q(0, L), AF.Copy)
        for h in (1, 0):
            cp(SI(h, 8, 16), RW("R0S", h, 8 * t, 8 * t + 8))
            if t:
                r = (0, nh[h])
                k = lambda a: A("KEY%d" % h, a, a + 8, 1, r)
                nf = hc("NF", h, nh[h])
                ts(nf, k(168), 0.0, OP.is_equal)
                tt(nf, nf, A("R0S_%d" % h, 8 * t, 8 * t + 8, 1, r), OP.mult)
                tt(A("SI", 16 * h + 8, 16 * h + 16, 1, r), k(152), nf, OP.add)
                ts(hc("NB", h, nh[h]), k(160), -1.0, OP.mult)
        if t == 0:
            for a, b in ((0, 1152), (1152, CW)):
                ts(A("CH", a, b), A("CHI", a, b), A("C4K"), OP.add)
            fill(A("PT", 0, 1), 256.0)
        for h in (1, 0):
            k = NL[h] // 16
            kids(h, 1.0)
            a0 = HB("A0", h, 0, NL[h])
            tt(a0, ind(A("PT"), HB("LT", h, 0, k)), q(K0[h], K0[h] + NL[h]), OP.subtract)
            act(a0, a0, AF.Abs)
            mm(RW("KEY", h, 144, 152), a0, A("R8"))
        for h in (1, 0):
            cp(SI(h, 0, 8), RW("KEY", h, 144, 152))
            ts(RW("ST", h), SI(h, 0, 16), 1.0 / 65536, OP.mult)
            masks(h, 0, True, [])
            tt(RW("SEL", h), SI(h, 0, 8), SI(h, 8, 16), OP.is_lt)
            tt(RW("RBC", h), SI(h, 0, 8), SI(h, 8, 16), OP.min)
            tt(HI(h, 1), RW("SEL", h), RW("ROOT", h), OP.mult)
        for h in (1, 0):
            points(h)
            keys(h)
        for s in range(1, ST + 2):
            for h in (1, 0):
                half[0] = h
                look(h, s)
            if s <= ST:
                for h in (1, 0):
                    half[0] = h
                    kids(h)
                    points(h)
                    keys(h)
                    fallback(h, FBS.get(s, []))
        half[0] = 0

        last = t == VI - 1
        both = lambda nm: A(nm, 0, 16)
        if not last:
            for h in (1, 0):
                tt(hc("FAR", h), HI(h, 7), A("TH", 0, 8, 1, (0, NL[h])), OP.is_ge)
            mm(RW("FB", 0, 0, 8), EYE("TRI", 112), hc("FAR", 0))
            mm(RW("FB", 1, 0, 8), EYE("TRI", 96), hc("FAR", 1), True, False)
            mm(RW("FB", 1, 0, 8), A("ONB", 0, 96, 1, (0, 112)), hc("FAR", 0), False, True)
            for h in (1, 0):
                ts(hc("S0", h), RW("FB", h, 0, 8), float(CAP - 512), OP.is_lt)
                tt(hc("DB", h), RW("FB", h, 0, 8), hc("KC2", h), OP.add)
            tt(both("DB"), both("DB"), both("S0"), OP.mult)
            tt(both("DST"), both("KC"), both("DB"), OP.add)
            for h in (1, 0):
                to_list(A("DST", 8 * h, 8 * h + 8), h)
        ts(both("LWL"), A("H", 7, 128, 8), 4095, OP.bitwise_and)
        ts(A("LW"), A("H"), 4095, OP.bitwise_and)
        ts(A("LD0"), A("LW"), 0, OP.is_equal)
        cp(A("LF"), A("LW"))
        cp(A("LF", 0, 128, 8), both("NB"))
        scan(A("LS"), A("LD0"), A("LF"), OP.mult, OP.add)
        res = A("LS", 6, 128, 8)
        ts(both("N1"), res, 0.0, OP.max)
        ts(both("B1"), res, 0.0, OP.is_gt, 4096.0 * rank, OP.mult)
        tt(both("B1"), both("B1"), both("N1"), OP.add)
        tt(both("B1"), both("B1"), both("N1"), OP.add)
        tt(both("B1"), both("B1"), res, OP.subtract)
        ts(both("Z1"), both("LWL"), 0, OP.is_equal)
        tt(both("N1"), both("N1"), both("Z1"), OP.mult)
        tt(both("NOD"), both("N1"), both("LWL"), OP.add)
        tt(both("B1"), both("B1"), both("Z1"), OP.mult)
        ts(both("Z1"), both("Z1"), -4096.0 * rank, OP.mult, 4096.0 * rank, OP.add)
        tt(both("B1"), both("B1"), both("LWL"), OP.add)
        tt(both("BST"), both("B1"), both("Z1"), OP.add)
        if not last:
            for h in (1, 0):
                list_copy(A("DL", 7 * h, 7 * h + NL[h] // 16), h)
            w1, w2 = (ind(A("SEND%d" % t, a, a + 368), A("DL", 0, 13)) for a in (0, 368))
            cp(w1, q(0, L))
            for h in (1, 0):
                ts(A("MI", 128 * h, 128 * h + 128, 16, (0, NL[h])), SI(h, 8, 16), 16, OP.logical_shift_right)
            cp(both("BEST"), both("BST"))
            ts(A("MI", 1, 256, 16), both("BEST"), 63, OP.bitwise_and)
            ts(A("MI", 2, 256, 16), both("BEST"), 6, OP.logical_shift_right, 63, OP.bitwise_and)
            ts(A("MI", 3, 256, 16), both("BEST"), 12, OP.logical_shift_right)
            cp(A("ML"), A("MI"))

            def to_gp(z="ZB0", ml="ML"):
                for h in (1, 0):
                    mm(A(z, K0[h], K0[h] + NL[h]), A(ml, 128 * h, 128 * h + 128, 1, (0, NL[h])), EYE("IB", NL[h]))
            to_gp()
            act(A("MG"), A("ZB0", 0, L), AF.Copy)
            cp(w2, A("MG"))
            dst = cores[(rank + 1) % n]
            hop = hop_of(core, dst, cores, topo)
            rid, pid = topo.addr(hop, core)
            m = some(topo.engines(core, hop))

            def send(x, a, b):
                s, d = A("SEND%d" % t, a, a + CAP), A("LAND%d" % t, b, b + CAP)
                ra, rl = T.sem["a%s%d" % (x, t)], T.sem["l%s%d" % (x, t)]
                op("g", lambda: g.remote_dma(d[0], s[0], ra, rl, pid, rid, m), [s], [], "r", rl, 8, 1.0)
            send("q", 208, 0)
            send("m", 576, CAP)
        for h in (1, 0):
            ts(A("OUTL", 16 * h, 16 * h + 8, 1, (0, NL[h])), SI(h, 8, 16), 1.0 / 65536, OP.mult)
            cp(A("OUTL", 16 * h + 8, 16 * h + 16, 1, (0, NL[h])), hc("BST", h))
            mm(A("ZB1", K0[h], K0[h] + NL[h], 1, (0, 16)), A("OUTL", 16 * h, 16 * h + 16, 1, (0, NL[h])), EYE("IF", NL[h]))
        yo = A("YO", t * L, t * L + L)
        act(yo, A("ZB1", 0, L, 1, (0, 16)), AF.Copy)
        dma("y", T.yr[:, t * L:t * L + L], A("YO", t * L, t * L + L, 1, (0, 8))[0], [yo], [])
        dma("y", T.yb[:, t * L:t * L + L], A("YO", t * L, t * L + L, 1, (8, 16))[0], [yo], [])
        if last:
            break
        for h in (1, 0):
            to_list(A("NOD", 8 * h, 8 * h + 8), h)
        cp(A("PT", M + t * L, M + t * L + L), q(0, L))
        for h in (1, 0):
            list_copy(A("NLT", 7 * h, 7 * h + NL[h] // 16), h)
        act(A("GG"), ind(A("CH"), A("NLT", 0, 13)), AF.Copy)
        for h in (1, 0):
            ts(RW("BI", h), HI(h, 7), 20, OP.logical_shift_right)
            tt(HB("OL", h), ind(HB("BI", h), A("BCL")), A("RI"), OP.is_equal)
            mm(A("ZB0", 256 + K0[h], 256 + K0[h] + NL[h]), RW("OL", h), EYE("IB", NL[h]))
        ob = A("ZB0", 256, 256 + L)
        ts(A("BN"), A("KN"), float(t * L), OP.add)
        tt(A("BN"), A("BN"), ob, OP.mult)
        ts(A("BX"), ob, A("C4K1"), OP.mult, -1.0, OP.add)
        tt(A("EE"), A("GG"), A("BX"), OP.is_equal)
        for h in (1, 0):
            mm(RW("SP", h, 0, 8), A("EE", K0[h], K0[h] + NL[h]), A("R8"))
        cp(both("NCI"), both("NOD"))
        ts(A("MCJ", 3, 256, 16), both("NCI"), 63, OP.bitwise_and)
        ts(A("MCJ", 4, 256, 16), both("NCI"), 6, OP.logical_shift_right)
        cp(A("ML2"), A("MCJ"))
        to_gp("ZB1", "ML2")
        act(A("MGN"), A("ZB1", 0, L), AF.Copy)
        ts(both("FARS"), both("FAR"), 1.0 / 65536, OP.mult)
        tt(both("LOF"), A("MCJ", 3, 256, 16), both("FARS"), OP.mult)
        tt(both("HIF"), A("MCJ", 4, 256, 16), both("FARS"), OP.mult)
        tt(both("YPL"), both("FARS"), both("NOD"), OP.mult)
        for h in (1, 0):
            for j, nm in ((1, "LOF"), (2, "HIF")):
                tt(A("ML3", 128 * h + j, 128 * h + 128, 16, (0, NL[h])), RW("SP", h, 0, 8), hc(nm, h), OP.mult)
        to_gp("ZB0", "ML3")
        act(A("MG"), A("ZB0", 0, L), AF.Copy)
        for h in (1, 0):
            cp(hc("CAN", h), RW("SP", h, 0, 8))
        tt(both("YPL"), both("YPL"), both("CAN"), OP.mult)
        ts(both("DA"), both("YPL"), 0.0, OP.is_gt)
        tt(both("DA"), both("DA"), both("KJ"), OP.mult)
        tt(both("GD"), both("YPL"), both("DA"), OP.subtract)
        banks, z = ("FB0", "FB1", "ZB0", "ZB1"), 0
        for gr in range(8):
            lg = gr * L
            ts(A("LG", lg, lg + L), A("MGN"), A("GMF", gr, gr + 1), OP.mult)
            for h in (1, 0):
                nl, w = NL[h], K0[h] + NL[h]
                o = A(banks[z % 4], 0, w, 1, (0, nl))
                z += 1
                mm(o, A("LG", lg + K0[h], lg + w), A("MG", 0, w), True, False)
                mm(A(o[1], K0[h], w, 1, (0, nl)), EYE("IB", nl), A("TRP", 0, nl, 1, (0, nl)), False, True)
                least(A("DMIN", 8 * h + gr, 8 * h + gr + 1, 1, (0, nl)), o)
        ts(both("DMIN"), both("DMIN"), 0.0, OP.is_gt)
        tt(both("GD"), both("GD"), both("DMIN"), OP.mult)
        tt(both("DST"), both("KJ"), both("GD"), OP.add)
        tt(both("YPL"), both("YPL"), both("DMIN"), OP.mult)
        for h in (1, 0):
            to_list(A("DST", 8 * h, 8 * h + 8), h)
        for h in (1, 0):
            list_copy(A("DL2", 7 * h, 7 * h + NL[h] // 16), h)
        tt(ind(A("CH"), A("DL2", 0, 13)), A("GG"), A("BN"), OP.add)
        for h in (1, 0):
            mm(A("ZB1", K0[h], K0[h] + NL[h], 1, (0, 8)), hc("YPL", h), EYE("IF", NL[h]))
        yo = A("YPO", t * L, t * L + L)
        act(yo, A("ZB1", 0, L, 1, (0, 8)), AF.Copy)
        dma("y", T.yp[:, t * L:t * L + L], yo[0], [yo], [])

    if not PLAN:
        PLAN.update(plan(ops))
    emit(g, ops, QUE, SEM)


def plan(ops):
    def meets(a, b):
        if a[2] >= b[3] or b[2] >= a[3] or a[4] >= b[5] or b[4] >= a[5]:
            return False
        return not (a[6] == b[6] and a[6] > 1 and (a[4] - b[4]) % a[6] != 0)

    N = len(ops)
    tag = [o[0] if o[4] == "c" else "a%d" % i for i, o in enumerate(ops)]
    hist, deps, sent, pool = {}, [], [], []
    for i in range(N):
        R, Wr, kind, dep = ops[i][2], ops[i][3], ops[i][4], set()
        for lst, w in ((R, False), (Wr, True)):
            for r in lst:
                ps = r[1] in PSUMS
                for (j, rr, ww) in hist.get(r[1], []):
                    if j != i and ((ps and (tag[j] != tag[i] or w or ww)) or ((w or ww) and meets(r, rr))):
                        dep.add(j)
        if tag[i] == "g":
            dep.update(pool[-1:])
            pool.append(i)
        if kind == "x":
            dep.add(sent[-2 if ops[i - 1][4] != "x" else -1])
        if kind == "r":
            sent.append(i)
        deps.append(dep)
        for lst, w in ((R, False), (Wr, True)):
            for r in lst:
                h = hist.setdefault(r[1], [])
                if w and r[1] in PSUMS:
                    h[:] = []
                elif w and r[6] == 1:
                    h[:] = [e for e in h if not (r[2] <= e[1][2] and e[1][3] <= r[3] and r[4] <= e[1][4] and e[1][5] <= r[5])]
                h.append((i, r, w))
    after = [{"c": 0.18, "d": 2.2, "r": 6.0, "x": 0.1}[o[4]] for o in ops]
    nxt = [[] for _ in range(N)]
    for i in range(N):
        for j in deps[i]:
            nxt[j].append((i, tag[i] == tag[j] == "t"))
    way = [0.0] * N
    for i in range(N - 1, -1, -1):
        way[i] = ops[i][7] + after[i] + max([way[k] for k, st in nxt[i]] or [0.0])
    best = None
    for bias, noise, hold, seed in TRIES:
        order, when, end = in_time(ops, deps, nxt, after, way, bias, noise, hold, seed)
        if best is None or end < best[0]:
            best = (end, order, when)
    order, when = best[1], best[2]
    seq, num = {q: 0 for q in "vstg"}, [1] * N
    known = {q: {} for q in "vstgyx"}
    snap, need, waits = [None] * N, set(), [None] * N
    for i in order:
        q = ops[i][0]
        if ops[i][4] == "c":
            seq[q] += 1
            num[i] = seq[q]
        k, mine, last = known[q], [], {}
        for j in deps[i]:
            if ops[i][4] == "x" or tag[j] == tag[i] == "t":
                continue
            if tag[j] not in last or num[last[tag[j]]] < num[j]:
                last[tag[j]] = j
        for j in sorted(last.values(), key=lambda j: -when[j]):
            if k.get(tag[j], 0) >= num[j]:
                continue
            mine.append(j)
            need.add(j)
            for a, b in snap[j].items():
                if k.get(a, 0) < b:
                    k[a] = b
        waits[i] = mine
        snap[i] = dict(k)
        snap[i][tag[i]] = num[i]
    return {"order": order, "waits": waits, "need": need}


def in_time(ops, deps, nxt, after, way, bias, noise, hold, seed):
    N = len(ops)
    left = [len(d) for d in deps]
    when = [0.0] * N
    free = {q: 0.0 for q in "vstgyx"}
    ready = {q: [i for i in range(N) if ops[i][0] == q and left[i] == 0] for q in free}
    z, pr = seed, []
    for i in range(N):
        z = (1103515245 * z + 12345) % 2147483648
        pr.append(way[i] + bias * ops[i][8] + noise * z / 2147483648.0)
    order = []
    while len(order) < N:
        best = None
        for q in free:
            if ready[q]:
                t = max(free[q], min(when[i] for i in ready[q]))
                if best is None or t < best[0]:
                    best = (t, q)
        t, q = best
        i = max((i for i in ready[q] if when[i] <= t + hold), key=lambda k: (pr[k], -k))
        ready[q].remove(i)
        free[q] = max(t, when[i]) + ops[i][7]
        end = free[q] + after[i]
        order.append(i)
        for k, st in nxt[i]:
            left[k] -= 1
            when[k] = max(when[k], free[q] if st else end)
            if left[k] == 0:
                ready[ops[k][0]].append(k)
    return order, when, max(free.values())


def emit(g, ops, QUE, SEM):
    cnt, at = {q: 0 for q in "vstg"}, {}
    for i in PLAN["order"]:
        q, fn, R, Wr, kind, sem, val = ops[i][:7]
        if kind == "x":
            continue
        for j in PLAN["waits"][i]:
            s, v = at[j] if j in at else (ops[j][5], ops[j][6])
            QUE[q].wait_ge(s, v)
        inst = fn()
        if kind == "d":
            inst.then_inc(sem, val)
        elif kind == "c" and i in PLAN["need"]:
            cnt[q] += 1
            inst.then_inc(SEM[q], 1)
            at[i] = (SEM[q], cnt[q])
    for q in cnt:
        if cnt[q]:
            g.wait_ge(SEM[q], cnt[q])
    for o in ops:
        if o[4] in ("d", "r", "x"):
            g.wait_ge(o[5], o[6])
